import numpy as np, ml_dtypes
CORES = [113,118,241,246]
N = 4
BF = ml_dtypes.bfloat16
def gentries(a):
    return np.ascontiguousarray(a.reshape(8, 16, -1).transpose(0, 2, 1)).reshape(8, -1)
def gtable(e):
    e = np.asarray(e); return np.ascontiguousarray(e.reshape(8, -1, 16).transpose(0, 2, 1)).reshape(128, -1).astype(np.int32)
S, V, RO, C = 1, 2560, 4, 10
def pairs(rng, F):
    o = np.argsort(rng.random((N, 8, RO, S, V)), axis=-1)
    w = np.ascontiguousarray(o.reshape(N, 8, RO, S, V // 2, 2)[..., ::-1]).reshape(N, 8, RO, S, V)
    w[..., :F] = o[..., :F]
    m = np.empty_like(o); np.put_along_axis(m, o, w, -1)
    return m
def whole_in(rng, size):
    return np.rint(size * (2.0 * rng.random((N, 8, 16, S, V)) - 1.0)).astype(np.int64)
def parts(rng):
    x = whole_in(rng, rng.choice(np.array([3.0, 10.0, 30.0, 60.0]), (N, 8, 1, S, V)))
    p = np.argsort(rng.random((N, 8, S, V)), axis=-1)
    return x, p, pairs(rng, 2 * (V // 64))
def pack(x, p, m):
    return {"x": np.ascontiguousarray(x.reshape(N, 128, S * V)).astype(np.float32).astype(BF),
            "p": np.stack([gtable(a.reshape(8, -1)) for a in p]), "mate": np.stack([gtable(a.reshape(8, -1)) for a in m])}
def put(x, p, m, g, xs, ps, ms):
    x[:, g] = xs.reshape(N, S, 16, V).transpose(0, 2, 1, 3)
    p[:, g] = ps.reshape(N, S, V)
    m[:, g, :len(ms)] = np.reshape(ms, (-1, N, S, V)).transpose(1, 0, 2, 3)
def sides(rng):
    Z = N * S; h = V // 2
    o = np.argsort(rng.random((Z, V)), axis=-1)
    b = np.empty((Z, V), np.int64); ps = np.empty((Z, V), np.int64); ms = np.empty((Z, V), np.int64)
    np.put_along_axis(b, o, np.tile(np.where(np.arange(V) < h, 1, -1), (Z, 1)), 1)
    np.put_along_axis(ps, o, np.roll(o, -1, axis=0), 1)
    a = o[:, :h]; c = np.take_along_axis(o[:, h:], np.argsort(rng.random((Z, h)), axis=-1), 1)
    np.put_along_axis(ms, a, c, 1); np.put_along_axis(ms, c, a, 1)
    return b, ps, ms
def link(x, p, back, used, mt, z, a, e):
    b = back[z, e]; u = (z + 1) % (N * S)
    if used[z, a] or used[z, b]: return False
    if a != b:
        i = p[z, a]
        va, vb, vi, ve = x[z, :, a], x[z, :, b], x[u, :, i], x[u, :, e]
        if np.sum(np.abs(va - vi) + np.abs(vb - ve) - np.abs(va - ve) - np.abs(vb - vi)) <= 0: return False
        mt[z, a] = b; mt[z, b] = a
    used[z, a] = True; used[z, b] = True
    return True
def grow(rng):
    Z = N * S; h = C // 2
    x = rng.integers(-60, 61, (Z, 16, V))
    x[:, :4] = np.where(rng.random((Z, 1, V)) < 0.0625, 60 - h, 60) * np.array([1, 1, -1, 1])[None, :, None]
    p = np.argsort(rng.random((Z, V)), axis=-1); m = np.tile(np.arange(V), (RO, Z, 1)); x0 = x; p0 = p
    for t in range(RO):
        if t > 0:
            back = np.argsort(p, axis=-1); used = np.zeros((Z, V), bool); w = x[:, 0]; hi = 60 + t * h; want = 32 >> (t - 1)
            hot = [np.flatnonzero(w[z] == hi) for z in range(Z)]
            for z in range(Z):
                l = (z - 1) % Z; u = (z + 1) % Z
                for c in rng.permutation(np.flatnonzero(w[z] == hi - h))[:want]:
                    if any(link(x, p, back, used, m[t], l, e, c) for e in rng.permutation(hot[l])[:16]):
                        any(link(x, p, back, used, m[t], z, c, e) for e in rng.permutation(hot[u])[:16])
                if t < RO - 1:
                    for c in rng.permutation(np.flatnonzero((w[z] == 60) & (w[u][p[z]] >= 60) & ~used[z]))[:want]:
                        if not used[z, c] and any(link(x, p, back, used, m[t], l, e, c) for e in rng.permutation(hot[l])[:16]): used[z, c] = True
        p = np.take_along_axis(p, m[t], 1)
        succ = np.take_along_axis(np.roll(x, -1, axis=0), p[:, None, :], 2)
        pred = np.roll(np.take_along_axis(x, np.argsort(p, axis=-1)[:, None, :], 2), 1, axis=0)
        x = x + np.clip(pred + succ - 2 * x, -C, C)
    return x0, p0, m
def setup_inputs(rng):
    return pack(*parts(rng))
def setup_inputs_near(rng):
    x, p, m = parts(rng); x = whole_in(rng, 60.0)
    m[:, :, 0] = pairs(rng, 0)[:, :, 0]; m0 = m[:, :, 0]; ar = np.arange(V)
    x = np.take_along_axis(x, np.minimum(ar, m0)[:, :, None], 4)
    co = np.arange(16)[None, None, :, None, None]; late = (ar > m0)[:, :, None]
    for i in range(2):
        x = x + (rng.integers(0, 16, (N, 8, 1, S, V)) == co) * rng.integers(-3, 4, (N, 8, 1, S, V)) * late
    return pack(np.clip(x, -60, 60), p, m)
def setup_inputs_ties(rng):
    x, p, m = parts(rng)
    x = rng.integers(-1, 2, (N, 8, 16, S, V)) * (np.arange(16)[None, :] <= np.arange(8)[:, None])[None, :, :, None, None]
    return pack(x, p, m)
def setup_inputs_still(rng):
    x, p, m = parts(rng); i = np.arange(V)
    p[:, 0] = i; p[:, 1] = V - 1 - i; p[:, 2] = np.roll(i, 1); p[:, 7] = np.roll(i, -1)
    m[:, 0] = i; m[:, 1] = i ^ 1; m[:, 2] = V - 1 - i; m[:, 4] = m[:, 4, :1].copy(); m[:, 5, RO - 1] = i
    x[:, 3] = x[:1, 3, :, :1, :1].copy()
    return pack(x, p, m)
def setup_inputs_ends(rng):
    x, p, m = parts(rng)
    v = rng.choice(np.array([60, 60, 59, 50, 45]), (N, 8, 16, S, V)); x = np.where(rng.random((N, 8, 16, S, V)) < 0.5, v, -v)
    x[:, 0] = v[:, 0]
    x[:, 1] = 60 * (1 - 2 * (np.arange(N * S).reshape(N, 1, S, 1) & 1))
    x[:, 2] = v[:, 2] * (1 - 2 * rng.integers(0, 2, (N, 1, S, V)))
    Z = N * S; turn = (1 - 2 * (np.arange(Z) & 1))[:, None, None]; odd = (np.arange(Z) & 1)[:, None] == 1
    b, ps, ms = sides(rng)
    put(x, p, m, 3, b[:, None, :] * turn * rng.integers(50, 61, (Z, 16, V)), ps, ms[None])
    b, ps, ms = sides(rng)
    put(x, p, m, 4, b[:, None, :] * np.where(np.arange(16)[None, :, None] < 8, turn, 1) * rng.integers(57, 61, (Z, 16, V)), ps, ms[None])
    put(x, p, m, 5, *grow(rng))
    b, ps, ms = sides(rng); dip = (b > 0) == odd
    xs = rng.integers(-2, 3, (Z, 16, V))
    xs[:, :2] = b[:, None, :] * np.where(dip[:, None, :], 60 - C // 2 + rng.integers(0, 3, (Z, 2, V)), 60)
    xs[:, 2:4] = b[:, None, :] * turn * 60
    xs[:, 4] = rng.integers(-6, 7, (Z, V))
    put(x, p, m, 6, xs, ps, np.stack([np.tile(np.arange(V), (Z, 1)), ms]))
    return pack(x, p, m)
def setup_inputs_spread(rng):
    x, p, m = parts(rng)
    x = whole_in(rng, 60.0 * np.exp2(-rng.integers(0, 7, (N, 8, 1, S, V)).astype(np.float64)) * (rng.random((N, 8, 1, S, V)) > 0.0625))
    return pack(x, p, m)
def check_inputs(d):
    bad = []; i = np.arange(V)
    a = np.asarray(d["x"]).astype(np.float64)
    if not (np.all(np.abs(a) <= 60) and np.all(a == np.rint(a))): bad.append("x whole from -60 to 60")
    q = np.stack([gentries(b) for b in d["p"]]).reshape(N, 8, S, V)
    if not np.all(np.sort(q, axis=-1) == i): bad.append("p permutations")
    m = np.stack([gentries(b) for b in d["mate"]]).reshape(N, 8, RO, S, V).astype(np.int64)
    if np.min(m) < 0 or np.max(m) > V - 1: bad.append("range of mate")
    elif not np.all(np.take_along_axis(m, m, -1) == i): bad.append("mate of the mate")
    return bad
def reference(x, p, mate):
    Z = N * S
    X = x.astype(np.float32).astype(np.int32).reshape(N, 8, 16, S, V).transpose(0, 3, 1, 2, 4).reshape(Z, 8, 16, V)
    P = np.stack([gentries(a) for a in p]).astype(np.int64).reshape(N, 8, S, V).transpose(0, 2, 1, 3).reshape(Z, 8, V)
    M = np.stack([gentries(a) for a in mate]).astype(np.int64).reshape(N, 8, RO, S, V).transpose(2, 0, 3, 1, 4).reshape(RO, Z, 8, V)
    for rnd in range(RO):
        m = M[rnd]
        s = np.take_along_axis(np.roll(X, -1, axis=0), P[:, :, None, :], 3)
        t = np.take_along_axis(s, m[:, :, None, :], 3)
        D = np.add.reduce(np.abs(X - s), axis=2) - np.add.reduce(np.abs(X - t), axis=2)
        go = D + np.take_along_axis(D, m, 2) > 0
        P = np.where(go, np.take_along_axis(P, m, 2), P)
        succ = np.where(go[:, :, None, :], t, s)
        back = np.argsort(P, axis=-1)
        pred = np.roll(np.take_along_axis(X, back[:, :, None, :], 3), 1, axis=0)
        X = X + np.clip(pred + succ - 2 * X, -C, C)
    yx = X.reshape(N, S, 8, 16, V).transpose(0, 2, 3, 1, 4).reshape(N, 128, S * V)
    yp = P.reshape(N, S, 8, V).transpose(0, 2, 1, 3).reshape(N, 8, S * V)
    return {"yx": yx.astype(np.float32).astype(BF), "yp": np.stack([gtable(a) for a in yp]).astype(np.float32)}

@@ -1,0 +1,536 @@
+from concourse.mybir import AluOpType as ALU, ActivationFunctionType as ACT
+from concourse.bass import DstId, RemoteDMATransfer
+
+V = 2560
+K = V // 16
+RO = 4
+CL = 10.0
+SEG = [(0, 512), (512, 1024), (1024, 1536), (1536, 2048), (2048, 2304), (2304, 2560)]
+SEG0 = [(0, 512), (512, 1024), (1024, 1536), (1536, 2048), (2048, 2560)]
+VIA0, VIA = (0, 1), (0, 1, 2)
+HALF = V // 2
+HELPED = [(1280, 1792), (1792, 2304), (2304, 2560)]
+OWN = [(0, 512), (512, 1024), (1024, 1280)]
+E = 96
+PMC = (64, 10, 10, 10, 0, 0)
+SC1 = 112
+YS_NEAR, YS_FAR = (K, 144, 144, 136), (112, 96, 96, 96)
+
+SCRATCH = {}
+for _n in ["x0", "x1", "x2", "x3", "x4", "n0", "n1", "p0", "p1", "M1", "M2", "Dv", "Dm", "Y", "X2", "W", "G"]:
+    SCRATCH[_n] = ("sbuf", [128, V], "bfloat16")
+SCRATCH.update({
+    "U": ("sbuf", [128, V], "float32"),
+    "Pi": ("sbuf", [128, K], "int32"),
+    "Pf": ("sbuf", [128, (RO + 1) * K], "float32"),
+    "Pu": ("sbuf", [128, (RO + 1) * K], "uint16"),
+    "Pd": ("sbuf", [128, RO * 2 * K], "bfloat16"),
+    "Si": ("sbuf", [128, K], "int32"),
+    "Su": ("sbuf", [128, RO * K], "uint16"),
+    "Mi": ("sbuf", [128, RO * K], "int32"),
+    "Mu": ("sbuf", [128, RO * K], "uint16"),
+    "Fu": ("sbuf", [128, RO * K], "uint16"),
+    "PMu": ("sbuf", [128, K], "uint16"),
+    "dP": ("sbuf", [128, K], "float32"),
+    "dS": ("sbuf", [128, K], "float32"),
+    "Di": ("sbuf", [128, 2 * K], "int32"),
+    "Dg": ("sbuf", [128, 3 * 2 * K], "bfloat16"),
+    "Dr": ("sbuf", [128, 3 * 2 * K], "bfloat16"),
+    "Sg": ("sbuf", [128, RO * K], "uint16"),
+    "Bk": ("sbuf", [128, RO * 2 * K], "uint16"),
+    "B0": ("sbuf", [128, 2 * K], "uint16"),
+    "fa": ("sbuf", [128, K], "int32"),
+    "fb": ("sbuf", [128, K], "float32"),
+    "fc": ("sbuf", [128, K], "float32"),
+    "fd": ("sbuf", [128, K], "float32"),
+    "J": ("sbuf", [128, 144], "float32"),
+    "A1": ("sbuf", [128, 144], "float32"),
+    "A2": ("sbuf", [128, 128], "float32"),
+    "i16": ("sbuf", [128, K], "float32"),
+    "ic": ("sbuf", [128, K], "float32"),
+    "vv": ("sbuf", [128, K], "float32"),
+    "cw": ("sbuf", [128, K], "bfloat16"),
+    "iw": ("sbuf", [128, K], "bfloat16"),
+    "ip": ("sbuf", [128, 4], "int32"),
+    "iq": ("sbuf", [128, 4], "int32"),
+    "j4": ("sbuf", [128, 4], "float32"),
+    "a4": ("sbuf", [128, 4], "float32"),
+    "e4": ("sbuf", [128, 4], "float32"),
+    "pm": ("sbuf", [128, 4], "float32"),
+    "wt": ("sbuf", [128, 4], "float32"),
+    "Zs": ("sbuf", [128, 144], "bfloat16"),
+    "Za": ("sbuf", [128, 144], "bfloat16"),
+    "Zb": ("sbuf", [128, 144], "bfloat16"),
+    "Zp": ("sbuf", [128, 144], "bfloat16"),
+    "I": ("sbuf", [128, 128], "bfloat16"),
+    "nI": ("sbuf", [128, 128], "bfloat16"),
+})
+for _n in range(8):
+    SCRATCH["b%d" % _n] = ("psum", [128, 512], "float32")
+
+NDMA = 24
+SEMAPHORES = (["cV", "cA", "cP", "cG", "snt", "bk"] + ["d%d" % _n for _n in range(NDMA)]
+              + ["%s%d" % (_s, _n) for _s in ("xn", "xp", "sg", "dg", "h0_", "h1_", "h2_") for _n in range(RO)])
+
+
+def bits(lst):
+    m = 0
+    for e in lst:
+        m |= 1 << e
+    return m
+
+
+def helper_of(core, far, T, topo):
+    for c in topo.cores_of(core):
+        if T.rank_of(c) is None and topo.die(c) != topo.die(core) and topo.may_write(c, far):
+            return c
+    return None
+
+
+def near_engines(core, near, far, topo):
+    off = topo.engines(core, far)
+    return [e for e in topo.engines(core, near) if e not in off]
+
+
+def neighbours(rank, T, topo):
+    cores = list(T.cores)
+    core, prv, nxt = cores[rank], cores[(rank - 1) % len(cores)], cores[(rank + 1) % len(cores)]
+    far, near = (nxt, prv) if prv in topo.cores_of(core) else (prv, nxt)
+    return prv, nxt, far, near
+
+
+def emit(ops, g, T):
+    Q = {"V": g.vector, "A": g.scalar, "P": g.tensor, "G": g, "S": g.sync}
+    hist = {}
+    know = {q: 0 for q in Q}
+    last = {q: 0 for q in Q}
+    done = []
+    for n, o in enumerate(ops):
+        q = o["q"]
+        deps = set()
+        if q is not None:
+            for (b, c0, c1), wr in [(r, False) for r in o["rd"]] + [(r, True) for r in o["wr"]]:
+                for (m, a0, a1, w2) in hist.get(b, []):
+                    p = ops[m]
+                    shared_bank = SCRATCH[b][0] == "psum" and p["q"] != q
+                    if shared_bank or (a0 < c1 and c0 < a1 and (wr or w2)):
+                        if q == "P" and p["q"] == "P":
+                            continue
+                        if o["grp"] is not None and p["grp"] is o["grp"]:
+                            continue
+                        deps.add(m)
+        o["waits"] = []
+        for m in sorted(deps, reverse=True):
+            if know[q] >> m & 1:
+                continue
+            o["waits"].append(m)
+            ops[m]["used"] = True
+            if ops[m]["grp"] is not None:
+                ops[m]["grp"]["used"] = True
+                for k in ops[m]["grp"]["ops"]:
+                    know[q] |= done[k]
+            else:
+                know[q] |= done[m]
+        d = (know[q] if q is not None else 0) | (1 << n)
+        if o["kind"] == "c":
+            d |= last[q]
+            last[q] = d
+        done.append(d)
+        if o["kind"] != "r":
+            for r, wr in [(r, False) for r in o["rd"]] + [(r, True) for r in o["wr"]]:
+                h = hist.setdefault(r[0], [])
+                if wr:
+                    h[:] = [e for e in h if not (r[1] <= e[1] and e[2] <= r[2] and (
+                        (q is not None and know[q] >> e[0] & 1) or (q == "P" and ops[e[0]]["q"] == "P")))]
+                h.append((n, r[1], r[2], wr))
+    cnt = {}
+    for o in ops:
+        if o["kind"] == "c" and o["used"]:
+            s = "c" + o["q"]
+            cnt[s] = cnt.get(s, 0) + 1
+            o["tok"] = (s, cnt[s])
+        elif o["kind"] == "d":
+            o["tok"] = (o["grp"]["sem"], 16 * len(o["grp"]["ops"]))
+    sent = 0
+    for o in ops:
+        if o["q"] is None:
+            continue
+        e = Q[o["q"]]
+        for m in o["waits"]:
+            e.wait_ge(T.sem[ops[m]["tok"][0]], ops[m]["tok"][1])
+        ins = o["fn"](e)
+        if o["kind"] == "c" and o["used"]:
+            ins.then_inc(T.sem[o["tok"][0]], 1)
+        elif o["kind"] == "d":
+            ins.then_inc(T.sem[o["tok"][0]], 16)
+        elif o["kind"] == "r":
+            sent += o["n"]
+    g.wait_ge(T.sem.snt, sent)
+    seen = set()
+    for o in ops:
+        left = (o["kind"] == "d" and not o["grp"]["used"]) or (o["kind"] == "e" and not o["used"])
+        if left and o["tok"] not in seen:
+            seen.add(o["tok"])
+            g.wait_ge(T.sem[o["tok"][0]], o["tok"][1])
+
+
+def relay_program(g, core, rank, T, topo):
+    prv, nxt, far, near = neighbours(rank, T, topo)
+    rid, pid = topo.addr(far, core)
+    ne_in = len(near_engines(T.cores[rank], core, far, topo))
+    total = 0
+    for t in range(RO):
+        if far == prv:
+            seg, via = (SEG, VIA) if t else (SEG0, VIA0)
+            jobs = [((sum(seg[k]) // 2, seg[k][1]), "h%d_" % j, "n", "xn") for j, k in enumerate(via)]
+        else:
+            jobs = [((HALF, V), "h0_", "p", "xp")]
+        total += len(jobs)
+        for (a, b), come, buf, sem in jobs:
+            g.wait_ge(T.sem["%s%d" % (come, t)], ne_in)
+            g.remote_dma(T["%s%d" % (buf, t % 2)][:, a:b], T["x%d" % t][:, a:b], T.sem["%s%d" % (sem, t)], T.sem.snt,
+                         pid, rid, topo.mask(core, far))
+    g.wait_ge(T.sem.snt, total * len(topo.engines(core, far)))
+
+
+def rank_program(g, core, T, topo):
+    rank = T.rank_of(core)
+    if rank is None:
+        for r in range(len(T.cores)):
+            if helper_of(T.cores[r], neighbours(r, T, topo)[2], T, topo) == core:
+                relay_program(g, core, r, T, topo)
+        return
+    prv, nxt, far, near = neighbours(rank, T, topo)
+    hlp = helper_of(core, far, T, topo)
+    e_far = topo.engines(core, far)
+    e_in = near_engines(core, near, far, topo)
+    e_all = topo.engines(core, near)
+    e_nxt = e_far if nxt == far else e_in
+    n_far = len(topo.engines(far, core))
+    n_piece = n_far if nxt == far else len(topo.engines(nxt, core))
+    n_small = n_far if prv == far else len(near_engines(prv, core, neighbours(T.rank_of(prv), T, topo)[2], topo))
+    n_whole = 2 * n_far if prv == far else n_small
+    YS = YS_FAR if prv == far else YS_NEAR
+    C1 = sum(PMC)
+
+    ops = []
+    ngrp = [0]
+
+    def ap(r):
+        return T[r[0]][:, r[1]:r[2]]
+
+    def rec(q, kind, fn, rd, wr, grp=None, n=0, tok=None):
+        o = {"q": q, "kind": kind, "fn": fn, "rd": rd, "wr": wr, "grp": grp, "used": False, "n": n, "tok": tok}
+        if grp is not None:
+            grp["ops"].append(len(ops))
+        ops.append(o)
+
+    def group():
+        ngrp[0] += 1
+        return {"sem": "d%d" % (ngrp[0] - 1), "ops": [], "used": False}
+
+    def bank(b, n=512):
+        return ("b%d" % b, 0, n)
+
+    def src(r):
+        if len(r) == 2:
+            return ap(r[0]).indirect(ap(r[1])), [r[0], r[1]]
+        return ap(r), [r]
+
+    def tt(o, a, b, op):
+        pa, ra = src(a)
+        rec("V", "c", lambda e: e.tensor_tensor(ap(o), pa, ap(b), op), ra + [b], [o])
+
+    def ts(o, a, s1, s2, op0, op1=None):
+        if op1 is None:
+            rec("V", "c", lambda e: e.tensor_scalar(ap(o), ap(a), s1, None, op0), [a], [o])
+        else:
+            rec("V", "c", lambda e: e.tensor_scalar(ap(o), ap(a), s1, s2, op0, op1), [a], [o])
+
+    def cp(o, a):
+        pa, ra = src(a)
+        rec("V", "c", lambda e: e.tensor_copy(ap(o), pa), ra, [o])
+
+    def act(o, a, func=ACT.Copy, scale=None, bias=None):
+        pa, ra = src(a)
+        kw = {}
+        for name, val in (("scale", scale), ("bias", bias)):
+            if isinstance(val, tuple):
+                kw[name] = ap(val)
+                ra = ra + [val]
+            elif val is not None:
+                kw[name] = val
+        rec("A", "c", lambda e: e.activation(ap(o), pa, func, **kw), ra, [o])
+
+    def mm(b, w, r, start, stop):
+        rec("P", "c", lambda e: e.matmul(T["b%d" % b][:, 0:r[2] - r[1]], T[w][:], ap(r), start, stop),
+            [(w, 0, 128), r], [bank(b)])
+
+    def wrap(b, oc, z, s, c0, c1, start, stop):
+        for i in range(16):
+            rec("P", "c", lambda e, i=i: e.matmul(T["b%d" % b][:, oc:oc + c1 - c0], T[z][:, 15 - i:143 - i],
+                                                   T[s][:, 16 * c0 + i:16 * c1:16], start and i == 0,
+                                                   stop and i == 15),
+                [(z, 0, 144), (s, 16 * c0, 16 * c1)], [bank(b)])
+
+    def dma(q, o, i, rd, wr, grp):
+        rec(q, "d", lambda e: e.dma_start(o, i), rd, wr, grp)
+
+    def flatten(row, hi, lo, grp):
+        for d, r in enumerate((hi, lo)):
+            dma("S", T.W[row + d:128:16, :], ap(r), [r], [("W", 0, V)], grp)
+
+    def send(dst, engines, o, i, sem, after=()):
+        rid, pid = topo.addr(dst, core)
+        rec("G", "r", lambda e: e.remote_dma(ap(o), ap(i), T.sem[sem], T.sem.snt, pid, rid, bits(engines)),
+            [i] + list(after), [], n=len(engines))
+
+    def arrive(r, sem, n):
+        rec(None, "e", None, [], [r], tok=(sem, n))
+
+    def iota(o, pattern, base, mult):
+        if SCRATCH[o[0]][2] == "int32":
+            rec("G", "c", lambda e: e.iota(ap(o), pattern, base, mult), [], [o])
+        else:
+            rec("G", "c", lambda e: e.iota(ap(o), pattern, base, mult, allow_small_or_imprecise_dtypes=True), [], [o])
+
+    def send_piece(t, k, a, b):
+        x = ("x%d" % t, a, b)
+        via = VIA if t else VIA0
+        if prv == far and k in via:
+            c = (a + b) // 2
+            trs = []
+            for dst, engines, o, i, sem in ((prv, e_far, ("n%d" % (t % 2), a, c), (x[0], a, c), "xn%d" % t),
+                                            (hlp, e_in, (x[0], c, b), (x[0], c, b), "h%d_%d" % (via.index(k), t))):
+                rid, pid = topo.addr(dst, core)
+                trs.append(RemoteDMATransfer(dst_ids=[DstId(rid=rid, pnc=pid)], dma_engine_mask=bits(engines),
+                                             remote_sem=T.sem[sem], src=ap(i), dst=ap(o)))
+            rec("G", "r", lambda e: e.remote_dma_fused(trs, local_sem=T.sem.snt), [x], [], n=len(e_far) + len(e_in))
+        else:
+            send(prv, e_far if prv == far else e_all, ("n%d" % (t % 2), a, b), x, "xn%d" % t)
+
+    def send_forward(t, nseg, digits=None):
+        n, x, p = ("n%d" % (t % 2), 0, V), "x%d" % t, "p%d" % (t % 2)
+        arrive(n, "xn%d" % t, (nseg + (len(VIA if t else VIA0) if nxt == far else 0)) * n_piece)
+        if digits is not None:
+            send(nxt, e_nxt, ("Dr",) + digits, ("Dg",) + digits, "dg%d" % (t - 1), after=[n] if nxt == far else [])
+            arrive(("Dr",) + digits, "dg%d" % (t - 1), n_small)
+        if nxt == far:
+            send(hlp, e_in, (x, HALF, V), (x, HALF, V), "h0_%d" % t, after=[n])
+            send(nxt, e_far, (p, 0, HALF), (x, 0, HALF), "xp%d" % t)
+        else:
+            send(nxt, e_in, (p, 0, V), (x, 0, V), "xp%d" % t)
+        arrive((p, 0, V), "xp%d" % t, n_whole)
+
+    def places(t):
+        m = ("Mi", t * K, (t + 1) * K)
+        ts(("fa", 0, K), m, 4, None, ALU.arith_shift_right)
+        ts(("fc", 0, K), m, float(K), None, ALU.mult)
+        ts(("fb", 0, K), ("fa", 0, K), float(1 - 16 * K), None, ALU.mult)
+        tt(("fd", 0, K), ("fb", 0, K), ("fc", 0, K), ALU.add)
+        cp(("Fu", t * K, (t + 1) * K), ("fd", 0, K))
+
+    def link_digits(t, grp):
+        P, hi, lo = ("Pf", t * K, (t + 1) * K), ("Pd", 2 * t * K, (2 * t + 1) * K), ("Pd", (2 * t + 1) * K, (2 * t + 2) * K)
+        cp(hi, P)
+        tt(lo, P, hi, ALU.subtract)
+        flatten(2, hi, lo, grp)
+
+    def pm_gather(t, c0, c1):
+        act(("G", 16 * c0, 16 * c1), (("W", 0, V), ("Fu", t * K + c0, t * K + c1)))
+
+    def pm_wrap():
+        wrap(6, 0, "Zp", "G", 0, C1, True, True)
+        wrap(7, 0, "Zp", "G", C1, K, True, True)
+
+    def pm_lists(t):
+        cp(("PMu", 0, C1), bank(6, C1))
+        cp(("PMu", C1, K), bank(7, K - C1))
+        tt(("dP", 0, C1), bank(6, C1), ("Pf", t * K, t * K + C1), ALU.subtract)
+        tt(("dP", C1, K), bank(7, K - C1), ("Pf", t * K + C1, (t + 1) * K), ALU.subtract)
+        tt(("dS", 0, K), ("Mi", t * K, (t + 1) * K), ("vv", 0, K), ALU.subtract)
+
+    def scatter(c0, c1):
+        rec("V", "c", lambda e: e.tensor_copy(T.Y[:, 0:V].indirect(T.Pu[:, c0:c1]), T.W[:, 16 * c0:16 * c1]),
+            [("W", 16 * c0, 16 * c1), ("Pu", c0, c1)], [("Y", 0, V)])
+
+    dma("S", T.Pi[:], T.p[:], [], [("Pi", 0, K)], group())
+    for k in (0, 1, 3):
+        dma("A", T.x0[:, SEG0[k][0]:SEG0[k][1]], T.x[:, SEG0[k][0]:SEG0[k][1]], [], [("x0",) + SEG0[k]], group())
+    dma("S", T.Mi[:, 0:2 * K], T.mate[:, 0:2 * K], [], [("Mi", 0, 2 * K)], group())
+    for k in (2, 4):
+        dma("S", T.x0[:, SEG0[k][0]:SEG0[k][1]], T.x[:, SEG0[k][0]:SEG0[k][1]], [], [("x0",) + SEG0[k]], group())
+    iota(("ip", 0, 4), [[0, 4]], 0, 1)
+    iota(("ic", 0, K), [[1, K // 16], [0, 16]], 0, 0)
+    iota(("iw", 0, K), [[0, K // 16], [1, 16]], 0, 0)
+    iota(("j4", 0, 4), [[-1, 4]], 0, 0)
+    iota(("J", 0, 144), [[1, 144]], -15, -1)
+    iota(("i16", 0, K), [[16, K]], 0, 0)
+    for k, (a, b) in enumerate(SEG0):
+        send_piece(0, k, a, b)
+    send_forward(0, len(SEG0))
+    pm = ("pm", 0, 1)
+    ts(("iq", 0, 4), ("ip", 0, 4), 15, None, ALU.bitwise_and)
+    cp(("pm", 0, 4), ("iq", 0, 4))
+    rec("V", "c", lambda e: e.memset(T.W[:], 0.0), [], [("W", 0, V)])
+    act(("wt", 0, 1), pm, ACT.Identity, scale=float(K // 16))
+    act(("cw", 0, K), ("ic", 0, K), ACT.Identity, bias=("wt", 0, 1))
+    first = group()
+    flatten(0, ("cw", 0, K), ("iw", 0, K), first)
+    cp(("Pf", 0, K), ("Pi", 0, K))
+    link_digits(0, first)
+    cp(("Pu", 0, K), ("Pi", 0, K))
+    places(0)
+    places(1)
+    act(("a4", 0, 4), ("j4", 0, 4), ACT.Abs, bias=pm)
+    act(("A1", 0, 144), ("J", 0, 144), ACT.Abs, bias=pm)
+    act(("e4", 0, 4), ("a4", 0, 4), ACT.Relu, scale=-1.0, bias=1.0)
+    act(("Zs", 0, 144), ("A1", 0, 144), ACT.Relu, scale=-1.0, bias=1.0)
+    act(("wt", 1, 2), ("e4", 0, 1), ACT.Identity, scale=16.0, bias=("e4", 1, 2))
+    act(("wt", 2, 3), ("e4", 1, 2), ACT.Identity, scale=float(K), bias=("e4", 0, 1))
+    act(("wt", 3, 4), ("e4", 2, 3), ACT.Identity, bias=("e4", 3, 4))
+    act(("A2", 0, 128), ("J", 15, 143), ACT.Abs)
+    act(("Zp", 0, 144), ("Zs", 0, 144), ACT.Identity, scale=("wt", 3, 4))
+    act(("I", 0, 128), ("A2", 0, 128), ACT.Relu, scale=-1.0, bias=1.0)
+    act(("Za", 0, 144), ("Zs", 0, 144), ACT.Identity, scale=("wt", 1, 2))
+    act(("Zb", 0, 144), ("Zs", 0, 144), ACT.Identity, scale=("wt", 2, 3))
+    act(("nI", 0, 128), ("I", 0, 128), ACT.Identity, scale=-1.0)
+    act(("vv", 0, K), ("i16", 0, K), ACT.Identity, bias=pm)
+    scatter(0, SC1)
+    pm_gather(0, 0, C1)
+    pm_gather(0, C1, K)
+    pm_wrap()
+    act(("X2", 0, V), ("x0", 0, V), ACT.Identity, scale=-2.0)
+    pm_lists(0)
+    scatter(SC1, K)
+
+    for t in range(RO):
+        x, xo = "x%d" % t, "x%d" % (t + 1)
+        XN, XP = ("n%d" % (t % 2), 0, V), ("p%d" % (t % 2), 0, V)
+        P0, P1 = t * K, (t + 1) * K
+        more = t + 1 < RO
+
+        def m1(a, b):
+            tt(("M1", a, b), (XN, ("Pu", P0 + a // 16, P0 + b // 16)), (x, a, b), ALU.max)
+
+        def m2(a, b):
+            tt(("M2", a, b), (XN, ("PMu", a // 16, b // 16)), (x, a, b), ALU.max)
+
+        H, O = HELPED, OWN
+        hb = (6, 7, 2)
+        for j in range(3):
+            mm(hb[j], "nI", (x,) + H[j], True, False)
+        for j in range(2):
+            mm(j, "nI", (x,) + H[j], True, False)
+        for j in range(3):
+            act(("M2",) + H[j], (XN, ("PMu", H[j][0] // 16, H[j][1] // 16)))
+            m1(*H[j])
+            mm(hb[j], "I", ("M2",) + H[j], False, True)
+            if j < 2:
+                mm(j, "I", ("M1",) + H[j], False, False)
+        for j in range(3):
+            act(("Dm",) + H[j], bank(hb[j], H[j][1] - H[j][0]), ACT.Relu)
+        mm(0, "nI", ("Dm",) + H[0], False, True)
+        m1(*O[0])
+        mm(3, "I", ("M1",) + O[0], True, False)
+        mm(1, "nI", ("Dm",) + H[1], False, True)
+        m2(*O[0])
+        mm(3, "nI", ("M2",) + O[0], False, True)
+        mm(2, "nI", (x,) + H[2], True, False)
+        mm(2, "I", ("M1",) + H[2], False, False)
+        mm(2, "nI", ("Dm",) + H[2], False, True)
+        for j in range(3):
+            act(("Dv",) + H[j], bank(j, H[j][1] - H[j][0]))
+        act(("Dv",) + O[0], bank(3, O[0][1] - O[0][0]))
+        for j in (1, 2):
+            m1(*O[j])
+            mm(3 + j, "I", ("M1",) + O[j], True, False)
+            m2(*O[j])
+            mm(3 + j, "nI", ("M2",) + O[j], False, True)
+        act(("Dv",) + O[1], bank(4, O[1][1] - O[1][0]))
+        cp(("Mu", P0, P1), ("Mi", P0, P1))
+        cp(("Dv",) + O[2], bank(5, O[2][1] - O[2][0]))
+        wrap(7, 0, "Zs", "Dv", E, K, True, False)
+        if t == 0:
+            dma("S", T.Mi[:, 2 * K:RO * K], T.mate[:, 2 * K:RO * K], [("Mu", 0, K)], [("Mi", 2 * K, RO * K)], group())
+        wrap(6, 0, "Zs", "Dv", 0, E, True, False)
+        for lo, hi, bk in ((0, E, 6), (E, K, 7)):
+            mid = (lo + hi) // 2
+            cp(("Dm", 16 * lo, 16 * mid), (("Dv", 0, V), ("Mu", P0 + lo, P0 + mid)))
+            act(("Dm", 16 * mid, 16 * hi), (("Dv", 0, V), ("Mu", P0 + mid, P0 + hi)))
+            wrap(bk, 0, "Zs", "Dm", lo, hi, False, True)
+        for lo, hi, bk in ((0, E, 6), (E, K, 7)):
+            ts(("b1", lo, hi), bank(bk, hi - lo), 0.0, None, ALU.is_gt)
+            tt(("b1", K + lo, K + hi), ("b1", lo, hi), ("dS", lo, hi), ALU.mult)
+            if lo:
+                tt(("b1", 2 * K, 3 * K), ("b1", 0, K), ("dP", 0, K), ALU.mult)
+            tt(("Si", lo, hi), ("b1", K + lo, K + hi), ("vv", lo, hi), ALU.add)
+        cp(("Su", P0, P1), ("Si", 0, K))
+        send(nxt, e_nxt, ("Sg", P0, P1), ("Su", P0, P1), "sg%d" % t)
+        arrive(("Sg", P0, P1), "sg%d" % t, n_small)
+        tt(("Pf", P1, P1 + K), ("b1", 2 * K, 3 * K), ("Pf", P0, P1), ALU.add)
+        cp(("Pu", P1, P1 + K), ("Pf", P1, P1 + K))
+        b0 = t * 2 * K
+        if t == 0:
+            wrap(0, 0, "Za", "Y", 0, K, True, True)
+            wrap(0, K, "Zb", "Y", 0, K, True, True)
+        else:
+            act(("G", 0, V), (("W", 0, V), ("Bk", b0 - K, b0)))
+            wrap(6, 0, "Za", "G", 0, K, True, True)
+            if more:
+                wrap(7, 0, "Zb", "G", 0, K, True, True)
+        if more:
+            link_digits(t + 1, group())
+        else:
+            out = group()
+            dma("S", T.yp[:], T.Pf[:, P1:P1 + K], [("Pf", P1, P1 + K)], [], out)
+        u0 = 0 if t else 48
+        if t == 0:
+            tt(("U", 0, 16 * u0), (XN, ("Pu", P1, P1 + u0)), ("X2", 0, 16 * u0), ALU.add)
+            cp(("B0", 0, 2 * K), bank(0, 2 * K))
+            send(nxt, e_nxt, ("Bk", 0, 2 * K), ("B0", 0, 2 * K), "bk")
+            arrive(("Bk", 0, 2 * K), "bk", n_small)
+        tt(("U", 16 * u0, V), (XN, ("Pu", P1 + u0, P1 + K)), ("X2", 16 * u0, V), ALU.add)
+        if t:
+            cp(("Bk", b0, b0 + K), bank(6, K))
+        act(("Y", 0, 16 * YS[t]), (XP, ("Sg", P0, P0 + YS[t])))
+        if YS[t] < K:
+            cp(("Y", 16 * YS[t], V), (XP, ("Sg", P0 + YS[t], P1)))
+        for k, (a, b) in enumerate(SEG[:-1]):
+            mm(k, "I", (x, a, b), True, False)
+
+        def step(k):
+            a, b = SEG[k]
+            tt(("M1", a, b), (("Y", 0, V), ("Bk", b0 + a // 16, b0 + b // 16)), ("U", a, b), ALU.add)
+
+        step(0)
+        for k, (a, b) in enumerate(SEG):
+            if k + 1 < len(SEG):
+                step(k + 1)
+            ts(("M1", a, b), ("M1", a, b), -CL, CL, ALU.max, ALU.min)
+            if k == 1 and t and more:
+                cp(("Bk", b0 + K, b0 + 2 * K), bank(7, K))
+            if more and PMC[k]:
+                pm_gather(t + 1, sum(PMC[:k]), sum(PMC[:k + 1]))
+            if k + 1 < len(SEG):
+                mm(k, "I", ("M1", a, b), False, True)
+                act((xo, a, b), bank(k, b - a))
+            else:
+                tt((xo, a, b), ("M1", a, b), (x, a, b), ALU.add)
+            if more:
+                send_piece(t + 1, k, a, b)
+            else:
+                dma("S", T.yx[:, a:b], T[xo][:, a:b], [(xo, a, b)], [], out)
+        if more:
+            pm_gather(t + 1, C1, K)
+            pm_wrap()
+            ts(("Di", 0, K), ("Si", 0, K), 4, None, ALU.arith_shift_right)
+            ts(("Di", K, 2 * K), ("Si", 0, K), 15, None, ALU.bitwise_and)
+            cp(("Dg", b0, b0 + 2 * K), ("Di", 0, 2 * K))
+            send_forward(t + 1, len(SEG), (b0, b0 + 2 * K))
+            flatten(0, ("Dr", b0, b0 + K), ("Dr", b0 + K, b0 + 2 * K), group())
+            if t + 2 < RO:
+                places(t + 2)
+            ts(("X2", 0, V), (xo, 0, V), -2.0, None, ALU.mult)
+            pm_lists(t + 1)
+    emit(ops, g, T)

@@ -5,72 +5,76 @@ V = 2560
 K = V // 16
 RO = 4
 CL = 10.0
-SEG = [(0, 512), (512, 1024), (1024, 1536), (1536, 2048), (2048, 2304), (2304, 2560)]
-SEG0 = [(0, 512), (512, 1024), (1024, 1536), (1536, 2048), (2048, 2560)]
-VIA0, VIA = (0, 1), (0, 1, 2)
-HALF = V // 2
-HELPED = [(1280, 1792), (1792, 2304), (2304, 2560)]
-OWN = [(0, 512), (512, 1024), (1024, 1280)]
-E = 96
-PMC = (64, 10, 10, 10, 0, 0)
-SC1 = 112
-YS_NEAR, YS_FAR = (K, 144, 144, 136), (112, 96, 96, 96)
+NR = 4
+B = 128 // NR
+XIN = [(0, 1536), (1536, V)]
+ROUND = 1.5 * 2 ** 23
+E = 64
+EP = 64
+SC = 112
+PIECES = {
+    "pm": [(0, 32), (32, 64), (64, 112), (112, 160)],
+    "s": [(0, 64), (64, 96), (96, 160)],
+    "t": [(0, 32), (32, 64), (64, 96), (96, 128), (128, 144), (144, 160)],
+    "dm": [(0, 32), (32, 64), (64, 112), (112, 160)],
+    "u": [(0, 32), (32, 64), (64, 112), (112, 136), (136, 160)],
+    "z": [(0, 32), (32, 64), (64, 112), (112, 160)],
+    "g": [(0, 32), (32, 64), (64, 96), (96, 128), (128, 160)],
+    "y": [(0, 32), (32, 64), (64, 96), (96, 128), (128, 144), (144, 160)],
+}
+XP = [(0, 64), (64, 96), (96, 160)]
+OUT = [(0, 64), (64, 128), (128, 160)]
+FIRST = ("s0 pmu0 s1 s2 pmu1 dp0 t2 t3 t4 t5 dv3 dv4 dm0 dm2 go0 dp1 sa0 sb0 ch0 pf0 go1 su0 sa1 sb1 ch1 pu0 pf1 u1 su1 pu1 lo z2 u2 y0 y2 c1 c0 c2 e0 c3 y5 c4 g3+ c5 e4 e5",
+         "pm0 pm1 pm2 pm3 t0 t1 r0 r1 dv0 dv2 dv1 dv5 dm1 dm3 z0 hi z1 z3 u0 y1 y3 y4 u3 pm0+ e1 pm1+ e2 e3")
+MID = ("pmu0 s0 s1 pmu1 dp0 t2 s2 t3 t4 t5 dv3 dv4 dm0 dm2 go0 dp1 sa0 sb0 ch0 pf0 go1 su0 sa1 sb1 ch1 pu0 pf1 u1 su1 pu1 bn lo z2 u2 y0 y2 c1 c0 c2 e0 c3 bf y5 c4 g3+ c5 e4 e5",
+       "pm2 pm3 t0 g1 t1 r0 r1 g0 dv0 dv2 dv1 dv5 dm1 dm3 g2 z0 hi z1 z3 u0 y1 y3 y4 u3 pm0+ e1 pm1+ e2 e3")
+LAST = ("pmu0 s0 s1 pmu1 dp0 t2 s2 t3 t4 t5 dv3 dv4 dm0 dm2 go0 dp1 sa0 sb0 ch0 pf0 go1 su0 sa1 sb1 ch1 pu0 pf1 u1 su1 pu1 bn z2 u2 y0 y2 c1 c0 c2 e0 c3 y5 c4 c5 e4 e5",
+        "pm2 pm3 t0 g1 t1 r0 r1 g0 dv0 dv2 dv1 dv5 dm1 dm3 g2 z0 z1 z3 u0 y1 y3 y4 u3 e1 e2 e3")
+FIRST = ('pm0 bn s0 pmu0 s2 pmu1 s1 t2 t3 bf t5 t4 dv5 dv4 dp0 df0 dp1 go0 sa0 sb0 ch0 su0 pf0 go1 sa1 sb1 ch1 pu0 pf1 su1 u1 pu1 z2 lo y0 u3 c1 c0 e1 e0 c3 c5 c2 e5 c4 e2 e4 e3',
+         'pm1 pm3 pm2 t0 fa t1 fb r0 fc r1 dv0 dv2 dv3 dv1 dm2 dm1 z0 z1 z3 hi u0 y1 u2 y3 u4 y5 y2 y4 pm1+')
+MID = ('s0 pmu0 dp0 t1 t0 s1 pmu1 s2 t2 t3 t4 t5 dv4 dp1 df0 go0 sa0 sb0 ch0 pf0 su0 pu0 go1 u1 sa1 sb1 ch1 bn pf1 su1 hi z2 pu1 lo y0 u3 c1 c0 e1 e0 u4 c2 c3 e2 e3 c5 c4 e5 e4 bf',
+       'pm0 pm3 pm2 g0 g1 g2 g3 g4 dv0 dv1 dv2 dv3 dv5 dm2 dm1 z1 z0 u0 z3 y1 y2 fa u2 y3 fb y5 y4 fc pm1+')
+LAST = ('s0 pmu0 t1 t0 pmu1 s1 t2 s2 t3 t5 t4 dv5 dv4 df0 dp0 go0 sa0 sb0 ch0 pf0 su0 pu0 dp1 go1 sa1 sb1 ch1 u1 su1 z2 pf1 bn pu1 y0 u3 c1 c0 e0 c2 e2 c3 e3 c4 c5 e4 e5',
+        'pm0 pm3 pm2 g2 g4 g0 g3 dv0 dv1 g1 dv2 dv3 dm1 dm2 z0 u0 z1 z3 y1 u2 y2 y3 e1 u4 y4 y5')
+FIRST = ('pm0 bn s0 pmu0 s1 s2 pmu1 dp1 t2 t3 bf t4 t5 dp0 dv4 dv5 dm0 dm2 go0 sa0 sb0 ch0 su0 go1 pf0 sa1 sb1 ch1 pu0 pf1 su1 u1 z2 lo y5 pu1 y0 u3 c1 c0 e1 e0 c5 c3 c2 e5 e2 c4 e3 e4',
+         'pm1 pm3 pm2 t0 t1 fa r0 fb r1 fc dv0 dv2 dv1 dv3 dm1 dm3 z0 z1 u0 hi z3 y1 u4 u2 y3 y2 pm1+ y4')
+MID = ('pmu0 s0 t0 t1 s1 dp0 pmu1 s2 t2 t3 t5 t4 dp1 dv4 dm0 dm2 go0 sa0 sb0 ch0 pf0 su0 pu0 u1 go1 sa1 sb1 ch1 bn pf1 su1 pu1 z2 u3 lo y0 u4 c1 c0 e1 e0 c3 c2 c5 e3 c4 e2 e4 e5 bf',
+       'pm0 pm3 pm2 g0 g1 g3 g2 g4 dv1 dv0 dv2 dv3 dv5 dm1 dm3 z1 z0 u0 z3 hi y1 u2 y3 y2 y5 fa y4 fb pm1+ fc')
+LAST = ('s0 pmu0 t1 t0 pmu1 s1 t2 s2 t3 t5 t4 dp0 dv5 dv4 dp1 dm0 dm2 go0 sa0 sb0 ch0 su0 pf0 go1 pu0 sa1 sb1 u1 su1 ch1 bn pf1 z2 pu1 y0 u3 c1 c0 e0 c2 e2 c3 e3 c4 c5 e4 e5',
+        'pm0 pm2 pm3 g3 g2 g1 dv0 dv1 g0 dv2 g4 dv3 dm1 dm3 z0 z1 u0 z3 y1 u2 y2 y3 e1 u4 y4 y5')
+LINES = [FIRST, MID, MID, LAST]
+LU = {"P": 0, "F0": 1, "M0": 2, "F1": 3, "M1": 4, "F2": 5, "M2": 6, "F3": 7, "M3": 8, "Bn": 9, "Bf": 10}
+CYC, PEC, FIX, SEM = 0.9e-3, 0.6e-3, 0.06, 0.1
+GATHER, SCATTER = 1.5, 3.5
+DMA_ISSUE, DMA_FIX, DMA_RATE, REM_FIX, REM_RATE, REM_FIRST = 0.1, 1.8, 300e3, 2.0, 50e3, 3.0
+SLACK = 0.3
 
 SCRATCH = {}
-for _n in ["x0", "x1", "x2", "x3", "x4", "n0", "n1", "p0", "p1", "M1", "M2", "Dv", "Dm", "Y", "X2", "W", "G"]:
+for _n in ["x0", "x1", "x2", "x3", "x4", "p0", "p1", "p2", "p3", "M1", "M2", "Dv", "Dm", "Y", "U", "W", "Wp", "G", "Gp",
+           "Sc", "C", "Z"]:
     SCRATCH[_n] = ("sbuf", [128, V], "bfloat16")
-SCRATCH.update({
-    "U": ("sbuf", [128, V], "float32"),
-    "Pi": ("sbuf", [128, K], "int32"),
-    "Pf": ("sbuf", [128, (RO + 1) * K], "float32"),
-    "Pu": ("sbuf", [128, (RO + 1) * K], "uint16"),
-    "Pd": ("sbuf", [128, RO * 2 * K], "bfloat16"),
-    "Si": ("sbuf", [128, K], "int32"),
-    "Su": ("sbuf", [128, RO * K], "uint16"),
-    "Mi": ("sbuf", [128, RO * K], "int32"),
-    "Mu": ("sbuf", [128, RO * K], "uint16"),
-    "Fu": ("sbuf", [128, RO * K], "uint16"),
-    "PMu": ("sbuf", [128, K], "uint16"),
-    "dP": ("sbuf", [128, K], "float32"),
-    "dS": ("sbuf", [128, K], "float32"),
-    "Di": ("sbuf", [128, 2 * K], "int32"),
-    "Dg": ("sbuf", [128, 3 * 2 * K], "bfloat16"),
-    "Dr": ("sbuf", [128, 3 * 2 * K], "bfloat16"),
-    "Sg": ("sbuf", [128, RO * K], "uint16"),
-    "Bk": ("sbuf", [128, RO * 2 * K], "uint16"),
-    "B0": ("sbuf", [128, 2 * K], "uint16"),
-    "fa": ("sbuf", [128, K], "int32"),
-    "fb": ("sbuf", [128, K], "float32"),
-    "fc": ("sbuf", [128, K], "float32"),
-    "fd": ("sbuf", [128, K], "float32"),
-    "J": ("sbuf", [128, 144], "float32"),
-    "A1": ("sbuf", [128, 144], "float32"),
-    "A2": ("sbuf", [128, 128], "float32"),
-    "i16": ("sbuf", [128, K], "float32"),
-    "ic": ("sbuf", [128, K], "float32"),
-    "vv": ("sbuf", [128, K], "float32"),
-    "cw": ("sbuf", [128, K], "bfloat16"),
-    "iw": ("sbuf", [128, K], "bfloat16"),
-    "ip": ("sbuf", [128, 4], "int32"),
-    "iq": ("sbuf", [128, 4], "int32"),
-    "j4": ("sbuf", [128, 4], "float32"),
-    "a4": ("sbuf", [128, 4], "float32"),
-    "e4": ("sbuf", [128, 4], "float32"),
-    "pm": ("sbuf", [128, 4], "float32"),
-    "wt": ("sbuf", [128, 4], "float32"),
-    "Zs": ("sbuf", [128, 144], "bfloat16"),
-    "Za": ("sbuf", [128, 144], "bfloat16"),
-    "Zb": ("sbuf", [128, 144], "bfloat16"),
-    "Zp": ("sbuf", [128, 144], "bfloat16"),
-    "I": ("sbuf", [128, 128], "bfloat16"),
-    "nI": ("sbuf", [128, 128], "bfloat16"),
-})
+SLOTS = NR * NR + NR - 1
+_tr = [("tp", K, "float32"), ("tl", 2 * K, "int32"), ("tu", 6 * K, "uint16"), ("td", 6 * K, "bfloat16"),
+       ("tb", 2 * K, "uint16")]
+_tr += [("tx%d" % _k, _b - _a, "bfloat16") for _k, (_a, _b) in enumerate(XIN)]
+_tr += [("to%d" % _k, 16 * (_b - _a), "bfloat16") for _k, (_a, _b) in enumerate(OUT)]
+for _n, _c, _d in _tr:
+    SCRATCH[_n] = ("dram", [SLOTS, 128, _c // NR], _d)
+for _d, _l in (
+        ("int32", {"Po": K, "Pi": K, "Mo": RO * K, "ip": 8, "iq": 8}),
+        ("uint16", {"Ou": 11 * K, "Lu": 11 * K, "Su": K, "Pu": RO * K, "PMu": K, "Bn": RO * K, "Bf": RO * K}),
+        ("float32", {"Pf": (RO + 1) * K, "dP": K, "Mq": RO * K, "Mr": RO * K, "J": 144, "A1": 144, "A2": 128, "ic": K,
+                     "sF": 128, "vF": 128, "Bq": 2 * K, "j8": 8, "a8": 8, "e8": 8, "pm": 8, "wt": 8}),
+        ("bfloat16", {"Od": 12 * K, "Ld": 12 * K, "Pd": 2 * RO * K, "go": K, "Sd": 2 * K, "cw": K, "iw": K, "vd": 2 * K, "Mh": RO * K,
+                      "Zs": 144, "Za": 144, "nV": 128, "Bh": K, "Zp": 144, "I": 256, "nI": 128, "n2": 128, "kI": 128, "sI": 128,
+                      "nS": 128})):
+    for _n, _c in _l.items():
+        SCRATCH[_n] = ("sbuf", [128, _c], _d)
 for _n in range(8):
     SCRATCH["b%d" % _n] = ("psum", [128, 512], "float32")
 
-NDMA = 24
-SEMAPHORES = (["cV", "cA", "cP", "cG", "snt", "bk"] + ["d%d" % _n for _n in range(NDMA)]
-              + ["%s%d" % (_s, _n) for _s in ("xn", "xp", "sg", "dg", "h0_", "h1_", "h2_") for _n in range(RO)])
+NDMA = 70
+SEMAPHORES = (["cV", "cA", "cP", "cG", "snt"] + ["d%d" % _n for _n in range(NDMA)] + ["r" + _n[0] for _n in _tr])
 
 
 def bits(lst):
@@ -78,25 +82,6 @@ def bits(lst):
     for e in lst:
         m |= 1 << e
     return m
-
-
-def helper_of(core, far, T, topo):
-    for c in topo.cores_of(core):
-        if T.rank_of(c) is None and topo.die(c) != topo.die(core) and topo.may_write(c, far):
-            return c
-    return None
-
-
-def near_engines(core, near, far, topo):
-    off = topo.engines(core, far)
-    return [e for e in topo.engines(core, near) if e not in off]
-
-
-def neighbours(rank, T, topo):
-    cores = list(T.cores)
-    core, prv, nxt = cores[rank], cores[(rank - 1) % len(cores)], cores[(rank + 1) % len(cores)]
-    far, near = (nxt, prv) if prv in topo.cores_of(core) else (prv, nxt)
-    return prv, nxt, far, near
 
 
 def emit(ops, g, T):
@@ -174,363 +159,460 @@ def emit(ops, g, T):
             g.wait_ge(T.sem[o["tok"][0]], o["tok"][1])
 
 
-def relay_program(g, core, rank, T, topo):
-    prv, nxt, far, near = neighbours(rank, T, topo)
-    rid, pid = topo.addr(far, core)
-    ne_in = len(near_engines(T.cores[rank], core, far, topo))
-    total = 0
-    for t in range(RO):
-        if far == prv:
-            seg, via = (SEG, VIA) if t else (SEG0, VIA0)
-            jobs = [((sum(seg[k]) // 2, seg[k][1]), "h%d_" % j, "n", "xn") for j, k in enumerate(via)]
-        else:
-            jobs = [((HALF, V), "h0_", "p", "xp")]
-        total += len(jobs)
-        for (a, b), come, buf, sem in jobs:
-            g.wait_ge(T.sem["%s%d" % (come, t)], ne_in)
-            g.remote_dma(T["%s%d" % (buf, t % 2)][:, a:b], T["x%d" % t][:, a:b], T.sem["%s%d" % (sem, t)], T.sem.snt,
-                         pid, rid, topo.mask(core, far))
-    g.wait_ge(T.sem.snt, total * len(topo.engines(core, far)))
+def order(ops, lines):
+    n = len(ops)
+    deps = [dict() for _ in ops]
+    hist = {}
+    for i, o in enumerate(ops):
+        if o["kind"] == "e":
+            deps[i][o["after"]] = True
+        for r, wr in [(r, False) for r in o["rd"]] + [(r, True) for r in o["wr"]]:
+            h = hist.setdefault(r[0], [])
+            psum = SCRATCH[r[0]][0] == "psum"
+            for (m, a0, a1, w2) in h:
+                p = ops[m]
+                if m == i or o["kind"] == "e" or (o["grp"] is not None and p["grp"] is o["grp"]):
+                    continue
+                meet = a0 < r[2] and r[1] < a1 and (wr or w2)
+                if meet or psum:
+                    hard = not (p["q"] == o["q"] and (o["q"] == "P" or not meet))
+                    for k in (p["grp"]["ops"] if p["grp"] else [m]):
+                        deps[i][k] = deps[i].get(k, False) or hard
+            if o["kind"] != "r":
+                if wr and o["grp"] is None:
+                    h[:] = [e for e in h if not (r[1] <= e[1] and e[2] <= r[2])]
+                h.append((i, r[1], r[2], wr))
+    for line in lines:
+        for m, i in zip(line, line[1:]):
+            deps[i].setdefault(m, False)
+    after = [[] for _ in ops]
+    for i in range(n):
+        for m in deps[i]:
+            after[m].append(i)
+    left = [len(d) for d in deps]
+    topo = [i for i in range(n) if not left[i]]
+    for i in topo:
+        for j in after[i]:
+            left[j] -= 1
+            if not left[j]:
+                topo.append(j)
+    assert len(topo) == n
+    chain = [0.0] * n
+    for i in reversed(topo):
+        o = ops[i]
+        chain[i] = o["dur"] + max([chain[j] + (o["lat"] if deps[j][i] else 0.0) for j in after[i]] + [o["lat"]])
+    left = [len(d) for d in deps]
+    ready = [0.0] * n
+    free = {q: 0.0 for q in ["V", "A", "P", "G", "S", None]}
+    cand = {q: [] for q in free}
+    for i in range(n):
+        if not left[i]:
+            cand[ops[i]["q"]].append(i)
+    out = []
+    while len(out) < n:
+        t0, q = min((max(free[q], min(ready[i] for i in c)), q or "") for q, c in cand.items() if c)
+        q = q or None
+        i = max((i for i in cand[q] if ready[i] <= t0 + SLACK), key=lambda i: (chain[i], -i))
+        o = ops[i]
+        cand[q].remove(i)
+        end = max(free[q], ready[i]) + o["dur"]
+        if q:
+            free[q] = end
+        out.append(i)
+        for j in after[i]:
+            ready[j] = max(ready[j], end + (o["lat"] if deps[j][i] else 0.0))
+            left[j] -= 1
+            if not left[j]:
+                cand[ops[j]["q"]].append(j)
+    place = {m: k for k, m in enumerate(out)}
+    for grp in [o["grp"] for k, o in enumerate(ops) if o["grp"] is not None and o["grp"]["ops"][0] == k]:
+        grp["ops"][:] = [place[m] for m in grp["ops"]]
+    return [ops[m] for m in out]
+
+
+def engine_shares(rank, T, topo):
+    core = T.cores[rank]
+    others = [r for r in range(len(T.cores)) if r != rank]
+    far = [r for r in others if T.cores[r] not in topo.cores_of(core)]
+    share, taken = {}, []
+    for j, r in enumerate(far):
+        e = topo.engines(core, T.cores[r])
+        n = len(e) // len(far)
+        share[r] = e[j * n:(j + 1) * n]
+        taken += share[r]
+    for r in others:
+        if r not in far:
+            share[r] = [e for e in topo.engines(core, T.cores[r]) if e not in taken]
+    return share
 
 
 def rank_program(g, core, T, topo):
     rank = T.rank_of(core)
     if rank is None:
-        for r in range(len(T.cores)):
-            if helper_of(T.cores[r], neighbours(r, T, topo)[2], T, topo) == core:
-                relay_program(g, core, r, T, topo)
         return
-    prv, nxt, far, near = neighbours(rank, T, topo)
-    hlp = helper_of(core, far, T, topo)
-    e_far = topo.engines(core, far)
-    e_in = near_engines(core, near, far, topo)
-    e_all = topo.engines(core, near)
-    e_nxt = e_far if nxt == far else e_in
-    n_far = len(topo.engines(far, core))
-    n_piece = n_far if nxt == far else len(topo.engines(nxt, core))
-    n_small = n_far if prv == far else len(near_engines(prv, core, neighbours(T.rank_of(prv), T, topo)[2], topo))
-    n_whole = 2 * n_far if prv == far else n_small
-    YS = YS_FAR if prv == far else YS_NEAR
-    C1 = sum(PMC)
+    share = engine_shares(rank, T, topo)
+    others = sorted(share)
+    come = sum(len(engine_shares(r, T, topo)[rank]) for r in others)
+    up = (rank + 1) % NR
 
     ops = []
     ngrp = [0]
+    sends = []
+    lines = {q: [] for q in "VAGS"}
+    keep = ["VAGS"]
+    named = {}
 
     def ap(r):
         return T[r[0]][:, r[1]:r[2]]
 
-    def rec(q, kind, fn, rd, wr, grp=None, n=0, tok=None):
-        o = {"q": q, "kind": kind, "fn": fn, "rd": rd, "wr": wr, "grp": grp, "used": False, "n": n, "tok": tok}
+    def w(name, a, b):
+        return (name, 16 * a, 16 * b)
+
+    def sl(name, slot, a=0, b=K):
+        return (name, slot * K + a, slot * K + b)
+
+    def rec(q, kind, fn, rd, wr, dur, lat=SEM, grp=None, n=0, tok=None, after=None, name=None):
+        o = {"q": q, "kind": kind, "fn": fn, "rd": rd, "wr": wr, "grp": grp, "used": False, "n": n, "tok": tok,
+             "dur": dur, "lat": lat, "after": after, "name": name}
         if grp is not None:
             grp["ops"].append(len(ops))
+        if name is not None:
+            named[name] = len(ops)
+        elif q is not None and q in keep[0]:
+            lines[q].append(len(ops))
         ops.append(o)
 
     def group():
         ngrp[0] += 1
         return {"sem": "d%d" % (ngrp[0] - 1), "ops": [], "used": False}
 
-    def bank(b, n=512):
-        return ("b%d" % b, 0, n)
+    def bank(b, n=512, o=0):
+        return ("b%d" % b, o, o + n)
 
     def src(r):
         if len(r) == 2:
             return ap(r[0]).indirect(ap(r[1])), [r[0], r[1]]
         return ap(r), [r]
 
-    def tt(o, a, b, op):
+    def cost(o, a, cycles=1.0):
+        return FIX + CYC * max(64, (o[2] - o[1]) * (GATHER if len(a) == 2 else cycles))
+
+    def tt(o, a, b, op, name=None):
         pa, ra = src(a)
-        rec("V", "c", lambda e: e.tensor_tensor(ap(o), pa, ap(b), op), ra + [b], [o])
+        both = all(SCRATCH[r[0]][0] == "sbuf" for r in ra + [b])
+        rec("V", "c", lambda e: e.tensor_tensor(ap(o), pa, ap(b), op), ra + [b], [o], cost(o, a, 2.0 if both else 1.0),
+            name=name)
 
-    def ts(o, a, s1, s2, op0, op1=None):
-        if op1 is None:
-            rec("V", "c", lambda e: e.tensor_scalar(ap(o), ap(a), s1, None, op0), [a], [o])
-        else:
-            rec("V", "c", lambda e: e.tensor_scalar(ap(o), ap(a), s1, s2, op0, op1), [a], [o])
+    def ts(o, a, s1, s2, op0, op1=None, name=None):
+        more = [] if op1 is None else [op1]
+        rec("V", "c", lambda e: e.tensor_scalar(ap(o), ap(a), s1, s2, op0, *more), [a], [o], cost(o, a), name=name)
 
-    def cp(o, a):
+    def cp(o, a, name=None):
         pa, ra = src(a)
-        rec("V", "c", lambda e: e.tensor_copy(ap(o), pa), ra, [o])
+        rec("V", "c", lambda e: e.tensor_copy(ap(o), pa), ra, [o], cost(o, a), name=name)
 
-    def act(o, a, func=ACT.Copy, scale=None, bias=None):
+    def fill(buf):
+        rec("V", "c", lambda e: e.memset(T[buf][:], 0.0), [], [(buf, 0, V)], cost((buf, 0, V), (buf, 0, V), 0.5))
+
+    def act(o, a, func=ACT.Copy, scale=None, bias=None, name=None):
         pa, ra = src(a)
         kw = {}
-        for name, val in (("scale", scale), ("bias", bias)):
+        for key, val in (("scale", scale), ("bias", bias)):
             if isinstance(val, tuple):
-                kw[name] = ap(val)
+                kw[key] = ap(val)
                 ra = ra + [val]
             elif val is not None:
-                kw[name] = val
-        rec("A", "c", lambda e: e.activation(ap(o), pa, func, **kw), ra, [o])
+                kw[key] = val
+        rec("A", "c", lambda e: e.activation(ap(o), pa, func, **kw), ra, [o], cost(o, a), name=name)
 
-    def mm(b, w, r, start, stop):
-        rec("P", "c", lambda e: e.matmul(T["b%d" % b][:, 0:r[2] - r[1]], T[w][:], ap(r), start, stop),
-            [(w, 0, 128), r], [bank(b)])
+    def mm(b, wt, r, start, stop, o=0):
+        name, s = wt if isinstance(wt, tuple) else (wt, 0)
+        rec("P", "c", lambda e: e.matmul(T["b%d" % b][:, o:o + r[2] - r[1]], T[name][:, s:s + 128], ap(r), start, stop),
+            [(name, s, s + 128), r], [bank(b)], PEC * max(64, r[2] - r[1]), 2 * SEM)
 
     def wrap(b, oc, z, s, c0, c1, start, stop):
-        for i in range(16):
-            rec("P", "c", lambda e, i=i: e.matmul(T["b%d" % b][:, oc:oc + c1 - c0], T[z][:, 15 - i:143 - i],
-                                                   T[s][:, 16 * c0 + i:16 * c1:16], start and i == 0,
-                                                   stop and i == 15),
-                [(z, 0, 144), (s, 16 * c0, 16 * c1)], [bank(b)])
+        def four(e, i0):
+            for i in range(i0, i0 + 4):
+                ins = e.matmul(T["b%d" % b][:, oc:oc + c1 - c0], T[z][:, 15 - i:143 - i],
+                               T[s][:, 16 * c0 + i:16 * c1:16], start and i == 0, stop and i == 15)
+            return ins
+        for i0 in range(0, 16, 4):
+            rec("P", "c", lambda e, i0=i0: four(e, i0), [(z, 0, 144), (s, 16 * c0, 16 * c1)], [bank(b)],
+                4 * PEC * max(64, c1 - c0), 2 * SEM)
 
-    def dma(q, o, i, rd, wr, grp):
-        rec(q, "d", lambda e: e.dma_start(o, i), rd, wr, grp)
+    def dma(q, o, i, rd, wr, size, grp=None):
+        rec(q, "d", lambda e: e.dma_start(o, i), rd, wr, DMA_ISSUE, DMA_FIX + size / DMA_RATE, grp or group())
 
-    def flatten(row, hi, lo, grp):
-        for d, r in enumerate((hi, lo)):
-            dma("S", T.W[row + d:128:16, :], ap(r), [r], [("W", 0, V)], grp)
+    def flatten(win, row, lst, grp, q="S"):
+        dma(q, T[win][row:128:16, :], ap(lst), [lst], [(win, 0, V)], 256 * K, grp)
 
-    def send(dst, engines, o, i, sem, after=()):
-        rid, pid = topo.addr(dst, core)
-        rec("G", "r", lambda e: e.remote_dma(ap(o), ap(i), T.sem[sem], T.sem.snt, pid, rid, bits(engines)),
-            [i] + list(after), [], n=len(engines))
+    def slot(u):
+        return NR - 1 + NR * u
 
-    def arrive(r, sem, n):
-        rec(None, "e", None, [], [r], tok=(sem, n))
+    def stage(q, buf, i, rd, mine, kept, size, rows=slice(0, 128), grp=None):
+        a = slot(mine) - kept
+        dma(q, T[buf][a:a + NR, rows, :], i, rd, [(buf, a, a + NR)], size, grp)
+
+    def places(buf, a=0, b=NR, rows=slice(0, 128)):
+        return T[buf][slot(a):slot(b - 1) + 1:NR, rows, :]
+
+    def landed(buf, a=0, b=NR):
+        return [(buf, slot(u), slot(u) + 1) for u in range(a, b)]
+
+    def trade(bufs, mine, kept, size):
+        trs, rd = [], []
+        for r in others:
+            rid, pid = topo.addr(T.cores[r], core)
+            n = len(share[r]) // len(bufs)
+            for j, buf in enumerate(bufs):
+                part = slot(mine) - kept + (kept + r - rank) % NR
+                rd.append((buf, part, part + 1))
+                trs.append(RemoteDMATransfer(dst_ids=[DstId(rid=rid, pnc=pid)],
+                                             dma_engine_mask=bits(share[r][j * n:(j + 1) * n]),
+                                             remote_sem=T.sem["r" + bufs[0]], src=T[buf][part], dst=T[buf][slot(mine)]))
+        sends.append(len(ops))
+        rec("G", "r", lambda e: e.remote_dma_fused(trs, local_sem=T.sem.snt), rd, [],
+            0.3 + size / REM_RATE + (REM_FIRST if len(sends) == 1 else 0.0), REM_FIX,
+            n=sum(len(share[r]) for r in others))
+        rec(None, "e", None, [], [r for buf in bufs for u in range(NR) if u != mine for r in landed(buf, u, u + 1)],
+            0.0, 0.0, tok=("r" + bufs[0], come), after=sends[-1])
 
     def iota(o, pattern, base, mult):
-        if SCRATCH[o[0]][2] == "int32":
-            rec("G", "c", lambda e: e.iota(ap(o), pattern, base, mult), [], [o])
+        kw = {} if SCRATCH[o[0]][2] == "int32" else {"allow_small_or_imprecise_dtypes": True}
+        rec("G", "c", lambda e: e.iota(ap(o), pattern, base, mult, **kw), [], [o], 0.13 + 2 * CYC * (o[2] - o[1]))
+
+    def mate_digits(c, a, b):
+        n = K * (b - a)
+        ts(sl("Mq", a, 0, n), sl("Mo", a, 0, n), 1.0 / 16, -7.5 / 16, ALU.mult, ALU.add)
+        act(sl("Mr", a, 0, n), sl("Mq", a, 0, n), ACT.Identity, bias=("wt", 6, 7))
+        act(sl("Mh", a, 0, n), sl("Mr", a, 0, n), ACT.Identity, bias=("wt", 7, 8))
+        for t in range(a, b):
+            mm(t, "sF", sl("Mq", t), True, False, o=K)
+            mm(t, "nS", sl("Mh", t), False, True, o=K)
+            mm(t, "I", sl("Mh", t), True, False, o=2 * K)
+            mm(t, "nI", sl("vd", 0), False, True, o=2 * K)
+        for t in range(a, b):
+            act(sl(c + "d", 3 + 2 * t), bank(t, K, K), ACT.Identity, bias=("pm", 2, 3))
+            act(sl(c + "d", 2 + 2 * t), bank(t, K, 2 * K))
+            mm(t, "I", sl("Mh", t), True, False)
+            mm(t, "kI", sl("vd", 1), False, False)
+            mm(t, "kI", sl(c + "d", 3 + 2 * t), False, True)
+
+    def mate_lists(c, t):
+        cp(sl(c + "u", LU["M%d" % t]), sl("Mo", t))
+        cp(sl(c + "u", LU["F%d" % t]), bank(t, K))
+
+    def columns(b, c, o, t):
+        act(("Bq", 0, K), bank(b, K), ACT.Identity, scale=1.0 / 16, bias=("pm", 3, 4), name=(t, "fa"))
+        act(("Bq", K, 2 * K), ("Bq", 0, K), ACT.Identity, bias=("wt", 6, 7), name=(t, "fb"))
+        act(("Bh", 0, K), ("Bq", K, 2 * K), ACT.Identity, bias=("wt", 7, 8), name=(t, "fc"))
+        mm(c, "vF", ("Bq", 0, K), True, False, o=o)
+        mm(c, "nV", ("Bh", 0, K), False, False, o=o)
+        mm(c, "I", ("Bh", 0, K), False, True, o=o)
+
+    def scatter(a, b):
+        rec("V", "c", lambda e: e.tensor_copy(T.Y[:, 0:V].indirect(T.Ou[:, a:b]), T.Sc[:, 16 * a:16 * b]),
+            [w("Sc", a, b), ("Ou", a, b)], [("Y", 0, V)], FIX + CYC * SCATTER * 16 * (b - a))
+
+    def land_x(h, name):
+        (a, b), buf, grp = XIN[h], "tx%d" % h, group()
+        if name == "x0":
+            dma("S", T.x0[:, a:b], places(buf), landed(buf), [("x0", a, b)], 256 * (b - a), grp)
         else:
-            rec("G", "c", lambda e: e.iota(ap(o), pattern, base, mult, allow_small_or_imprecise_dtypes=True), [], [o])
+            dma("S", T.p0[B:128, a:b], places(buf, 0, NR - 1), landed(buf), [("p0", a, b)], 256 * (b - a), grp)
+            dma("S", T.p0[0:B, a:b], places(buf, NR - 1, NR), landed(buf), [("p0", a, b)], 256 * (b - a), grp)
 
-    def send_piece(t, k, a, b):
-        x = ("x%d" % t, a, b)
-        via = VIA if t else VIA0
-        if prv == far and k in via:
-            c = (a + b) // 2
-            trs = []
-            for dst, engines, o, i, sem in ((prv, e_far, ("n%d" % (t % 2), a, c), (x[0], a, c), "xn%d" % t),
-                                            (hlp, e_in, (x[0], c, b), (x[0], c, b), "h%d_%d" % (via.index(k), t))):
-                rid, pid = topo.addr(dst, core)
-                trs.append(RemoteDMATransfer(dst_ids=[DstId(rid=rid, pnc=pid)], dma_engine_mask=bits(engines),
-                                             remote_sem=T.sem[sem], src=ap(i), dst=ap(o)))
-            rec("G", "r", lambda e: e.remote_dma_fused(trs, local_sem=T.sem.snt), [x], [], n=len(e_far) + len(e_in))
-        else:
-            send(prv, e_far if prv == far else e_all, ("n%d" % (t % 2), a, b), x, "xn%d" % t)
-
-    def send_forward(t, nseg, digits=None):
-        n, x, p = ("n%d" % (t % 2), 0, V), "x%d" % t, "p%d" % (t % 2)
-        arrive(n, "xn%d" % t, (nseg + (len(VIA if t else VIA0) if nxt == far else 0)) * n_piece)
-        if digits is not None:
-            send(nxt, e_nxt, ("Dr",) + digits, ("Dg",) + digits, "dg%d" % (t - 1), after=[n] if nxt == far else [])
-            arrive(("Dr",) + digits, "dg%d" % (t - 1), n_small)
-        if nxt == far:
-            send(hlp, e_in, (x, HALF, V), (x, HALF, V), "h0_%d" % t, after=[n])
-            send(nxt, e_far, (p, 0, HALF), (x, 0, HALF), "xp%d" % t)
-        else:
-            send(nxt, e_in, (p, 0, V), (x, 0, V), "xp%d" % t)
-        arrive((p, 0, V), "xp%d" % t, n_whole)
-
-    def places(t):
-        m = ("Mi", t * K, (t + 1) * K)
-        ts(("fa", 0, K), m, 4, None, ALU.arith_shift_right)
-        ts(("fc", 0, K), m, float(K), None, ALU.mult)
-        ts(("fb", 0, K), ("fa", 0, K), float(1 - 16 * K), None, ALU.mult)
-        tt(("fd", 0, K), ("fb", 0, K), ("fc", 0, K), ALU.add)
-        cp(("Fu", t * K, (t + 1) * K), ("fd", 0, K))
-
-    def link_digits(t, grp):
-        P, hi, lo = ("Pf", t * K, (t + 1) * K), ("Pd", 2 * t * K, (2 * t + 1) * K), ("Pd", (2 * t + 1) * K, (2 * t + 2) * K)
-        cp(hi, P)
-        tt(lo, P, hi, ALU.subtract)
-        flatten(2, hi, lo, grp)
-
-    def pm_gather(t, c0, c1):
-        act(("G", 16 * c0, 16 * c1), (("W", 0, V), ("Fu", t * K + c0, t * K + c1)))
-
-    def pm_wrap():
-        wrap(6, 0, "Zp", "G", 0, C1, True, True)
-        wrap(7, 0, "Zp", "G", C1, K, True, True)
-
-    def pm_lists(t):
-        cp(("PMu", 0, C1), bank(6, C1))
-        cp(("PMu", C1, K), bank(7, K - C1))
-        tt(("dP", 0, C1), bank(6, C1), ("Pf", t * K, t * K + C1), ALU.subtract)
-        tt(("dP", C1, K), bank(7, K - C1), ("Pf", t * K + C1, (t + 1) * K), ALU.subtract)
-        tt(("dS", 0, K), ("Mi", t * K, (t + 1) * K), ("vv", 0, K), ALU.subtract)
-
-    def scatter(c0, c1):
-        rec("V", "c", lambda e: e.tensor_copy(T.Y[:, 0:V].indirect(T.Pu[:, c0:c1]), T.W[:, 16 * c0:16 * c1]),
-            [("W", 16 * c0, 16 * c1), ("Pu", c0, c1)], [("Y", 0, V)])
-
-    dma("S", T.Pi[:], T.p[:], [], [("Pi", 0, K)], group())
-    for k in (0, 1, 3):
-        dma("A", T.x0[:, SEG0[k][0]:SEG0[k][1]], T.x[:, SEG0[k][0]:SEG0[k][1]], [], [("x0",) + SEG0[k]], group())
-    dma("S", T.Mi[:, 0:2 * K], T.mate[:, 0:2 * K], [], [("Mi", 0, 2 * K)], group())
-    for k in (2, 4):
-        dma("S", T.x0[:, SEG0[k][0]:SEG0[k][1]], T.x[:, SEG0[k][0]:SEG0[k][1]], [], [("x0",) + SEG0[k]], group())
-    iota(("ip", 0, 4), [[0, 4]], 0, 1)
+    g1, g3, g4, g5, g6 = group(), group(), group(), group(), group()
+    stage("S", "tl", T.p[:], [], up, rank, 512 * K, slice(0, 64), g1)
+    stage("A", "tl", T.mate[:, 0:K], [], up, rank, 512 * K, slice(64, 128), g1)
+    dma("S", T.Po[:], T.p[:], [], [("Po", 0, K)], 512 * K)
+    dma("A", T.Mo[:, K:RO * K], T.mate[:, K:RO * K], [], [("Mo", K, RO * K)], 2048 * K)
+    iota(("ip", 0, 8), [[0, 8]], 0, 1)
     iota(("ic", 0, K), [[1, K // 16], [0, 16]], 0, 0)
     iota(("iw", 0, K), [[0, K // 16], [1, 16]], 0, 0)
-    iota(("j4", 0, 4), [[-1, 4]], 0, 0)
     iota(("J", 0, 144), [[1, 144]], -15, -1)
-    iota(("i16", 0, K), [[16, K]], 0, 0)
-    for k, (a, b) in enumerate(SEG0):
-        send_piece(0, k, a, b)
-    send_forward(0, len(SEG0))
+    iota(("j8", 0, 8), [[-1, 8]], 0, 0)
+    iota(("vd", 0, K), [[1, K]], 0, 0)
+    trade(["tl"], up, rank, 256 * K)
     pm = ("pm", 0, 1)
-    ts(("iq", 0, 4), ("ip", 0, 4), 15, None, ALU.bitwise_and)
-    cp(("pm", 0, 4), ("iq", 0, 4))
-    rec("V", "c", lambda e: e.memset(T.W[:], 0.0), [], [("W", 0, V)])
+    ts(("iq", 0, 8), ("ip", 0, 8), 15, None, ALU.bitwise_and)
+    cp(("pm", 0, 8), ("iq", 0, 8))
+    fill("Sc")
     act(("wt", 0, 1), pm, ACT.Identity, scale=float(K // 16))
     act(("cw", 0, K), ("ic", 0, K), ACT.Identity, bias=("wt", 0, 1))
-    first = group()
-    flatten(0, ("cw", 0, K), ("iw", 0, K), first)
-    cp(("Pf", 0, K), ("Pi", 0, K))
-    link_digits(0, first)
-    cp(("Pu", 0, K), ("Pi", 0, K))
-    places(0)
-    places(1)
-    act(("a4", 0, 4), ("j4", 0, 4), ACT.Abs, bias=pm)
-    act(("A1", 0, 144), ("J", 0, 144), ACT.Abs, bias=pm)
-    act(("e4", 0, 4), ("a4", 0, 4), ACT.Relu, scale=-1.0, bias=1.0)
-    act(("Zs", 0, 144), ("A1", 0, 144), ACT.Relu, scale=-1.0, bias=1.0)
-    act(("wt", 1, 2), ("e4", 0, 1), ACT.Identity, scale=16.0, bias=("e4", 1, 2))
-    act(("wt", 2, 3), ("e4", 1, 2), ACT.Identity, scale=float(K), bias=("e4", 0, 1))
-    act(("wt", 3, 4), ("e4", 2, 3), ACT.Identity, bias=("e4", 3, 4))
+    flatten("Sc", 0, ("cw", 0, K), g3)
+    flatten("Sc", 1, ("iw", 0, K), g3)
+    for h, (a, b) in enumerate(XIN):
+        stage("S", "tx%d" % h, T.x[:, a:b], [], rank, rank, 512 * (b - a))
+        trade(["tx%d" % h], rank, rank, 64 * (b - a))
+    ts(("wt", 6, 7), pm, 0.0, ROUND, ALU.mult, ALU.add)
+    ts(("wt", 7, 8), pm, 0.0, -ROUND, ALU.mult, ALU.add)
+    ts(("pm", 2, 3), pm, -1.0, 7.5, ALU.mult, ALU.add)
+    ts(("pm", 3, 4), pm, 0.0, -7.5 / 16, ALU.mult, ALU.add)
+    fill("Wp")
+    cp(sl("Ou", 0), ("Po", 0, K))
     act(("A2", 0, 128), ("J", 15, 143), ACT.Abs)
-    act(("Zp", 0, 144), ("Zs", 0, 144), ACT.Identity, scale=("wt", 3, 4))
+    act(("a8", 0, 8), ("j8", 0, 8), ACT.Abs, bias=pm)
+    act(("A1", 0, 144), ("J", 0, 144), ACT.Abs, bias=pm)
     act(("I", 0, 128), ("A2", 0, 128), ACT.Relu, scale=-1.0, bias=1.0)
+    act(("e8", 0, 8), ("a8", 0, 8), ACT.Relu, scale=-1.0, bias=1.0)
+    act(("Zs", 0, 144), ("A1", 0, 144), ACT.Relu, scale=-1.0, bias=1.0)
+    act(("I", 128, 256), ("A2", 0, 128), ACT.Relu, scale=-1.0, bias=1.0)
+    for name, scale in (("kI", K), ("sF", 16), ("nS", -16), ("nI", -1), ("n2", -2), ("sI", 16)):
+        act((name, 0, 128), ("I", 0, 128), ACT.Identity, scale=float(scale))
+    act(("vd", K, 2 * K), ("ic", 0, K), ACT.Identity, scale=0.0, bias=pm)
+    mate_digits("O", 1, RO)
+    act(("W", 0, V), ("Wp", 0, V))
+    scatter(0, SC)
+    act(("wt", 4, 5), ("e8", 0, 1), ACT.Identity, bias=("e8", 2, 3))
+    act(("wt", 5, 6), ("e8", 1, 2), ACT.Identity, bias=("e8", 3, 4))
+    act(("wt", 3, 4), ("e8", 4, 5), ACT.Identity, bias=("e8", 5, 6))
+    act(("wt", 1, 2), ("wt", 4, 5), ACT.Identity, scale=16.0, bias=("wt", 5, 6))
+    act(("vF", 0, 128), ("I", 0, 128), ACT.Identity, scale=float(V))
+    act(("nV", 0, 128), ("I", 0, 128), ACT.Identity, scale=-float(V))
+    act(("Zp", 0, 144), ("Zs", 0, 144), ACT.Identity, scale=("wt", 3, 4))
     act(("Za", 0, 144), ("Zs", 0, 144), ACT.Identity, scale=("wt", 1, 2))
-    act(("Zb", 0, 144), ("Zs", 0, 144), ACT.Identity, scale=("wt", 2, 3))
-    act(("nI", 0, 128), ("I", 0, 128), ACT.Identity, scale=-1.0)
-    act(("vv", 0, K), ("i16", 0, K), ACT.Identity, bias=pm)
-    scatter(0, SC1)
-    pm_gather(0, 0, C1)
-    pm_gather(0, C1, K)
-    pm_wrap()
-    act(("X2", 0, V), ("x0", 0, V), ACT.Identity, scale=-2.0)
-    pm_lists(0)
-    scatter(SC1, K)
+    for t in range(1, RO):
+        mate_lists("O", t)
+    dma("S", T.Pi[:], places("tl", rows=slice(0, 64)), landed("tl"), [("Pi", 0, K)], 512 * K)
+    dma("S", T.Mo[:, 0:K], places("tl", rows=slice(64, 128)), landed("tl"), [sl("Mo", 0)], 512 * K)
+    land_x(0, "x0")
+    cp(sl("Pf", 0), ("Pi", 0, K))
+    cp(sl("Ld", 0), ("Pi", 0, K))
+    tt(sl("Ld", 1), sl("Pf", 0), sl("Ld", 0), ALU.subtract)
+    for d in range(2):
+        flatten("Wp", 4 + d, sl("Ld", d), g5)
+    land_x(1, "x0")
+    land_x(0, "p0")
+    land_x(1, "p0")
+    mate_digits("L", 0, 1)
+    cp(sl("Lu", LU["P"]), ("Pi", 0, K))
+    scatter(SC, K)
+    mate_lists("L", 0)
+    keep[0] = "GS"
+    stage("S", "tu", T.Ou[:, 3 * K:9 * K], [("Ou", 3 * K, 9 * K)], up, rank, 1536 * K, grp=g6)
+    stage("S", "td", T.Od[:, 4 * K:10 * K], [("Od", 4 * K, 10 * K)], up, rank, 1536 * K, grp=g6)
+    trade(["tu", "td"], up, rank, 768 * K)
+    wrap(4, 0, "Za", "Y", 0, K, True, True)
+    cp(sl("Ou", LU["Bn"]), bank(4, K), name=(0, "bn"))
+    columns(4, 5, 0, 0)
+    ts(sl("Ou", LU["Bf"]), bank(5, K), 7.5 * K, None, ALU.add, name=(0, "bf"))
+    stage("S", "tb", T.Ou[:, 9 * K:11 * K], [("Ou", 9 * K, 11 * K)], up, rank, 512 * K)
+    trade(["tb"], up, rank, 128 * K)
+    flatten("W", 2, ("vd", 0, K), g4)
+    flatten("W", 3, ("vd", K, 2 * K), g4)
+    dma("S", T.Lu[:, 9 * K:11 * K], places("tb"), landed("tb"), [("Lu", 9 * K, 11 * K)], 512 * K)
+    dma("S", T.Lu[:, 3 * K:9 * K], places("tu"), landed("tu"), [("Lu", 3 * K, 9 * K)], 1536 * K)
+    dma("S", T.Ld[:, 4 * K:10 * K], places("td"), landed("td"), [("Ld", 4 * K, 10 * K)], 1536 * K)
 
     for t in range(RO):
-        x, xo = "x%d" % t, "x%d" % (t + 1)
-        XN, XP = ("n%d" % (t % 2), 0, V), ("p%d" % (t % 2), 0, V)
-        P0, P1 = t * K, (t + 1) * K
+        x, xo, xp = "x%d" % t, "x%d" % (t + 1), "p%d" % t
+        X = (x, 0, V)
         more = t + 1 < RO
+        P, Bn = (("Pu", t - 1), ("Bn", t)) if t else (("Lu", LU["P"]), ("Lu", LU["Bn"]))
+        Bf = ("Bf", t) if t > 1 else ("Lu", LU["Bf"])
+        F, M = ("Lu", LU["F%d" % t]), ("Lu", LU["M%d" % t])
+        parts = [p for p in ((0, E, 0), (E, K, 1)) if p[0] < p[1]]
+        mine = LINES[t][0].split() + [n[:-1] for n in LINES[t - 1][0].split() if t and n[-1] == "+"]
 
-        def m1(a, b):
-            tt(("M1", a, b), (XN, ("Pu", P0 + a // 16, P0 + b // 16)), (x, a, b), ALU.max)
+        def on(name):
+            return cp if name in mine else act
 
-        def m2(a, b):
-            tt(("M2", a, b), (XN, ("PMu", a // 16, b // 16)), (x, a, b), ALU.max)
+        def gathers(kind, out, win, lst, lo=0, hi=K):
+            for k, (a, b) in enumerate(PIECES[kind]):
+                if lo <= a < hi:
+                    name = "%s%d" % (kind, k)
+                    on(name)(w(out, a, b), ((win, 0, V), sl(lst[0], lst[1], a, b)), name=(t, name))
 
-        H, O = HELPED, OWN
-        hb = (6, 7, 2)
-        for j in range(3):
-            mm(hb[j], "nI", (x,) + H[j], True, False)
-        for j in range(2):
-            mm(j, "nI", (x,) + H[j], True, False)
-        for j in range(3):
-            act(("M2",) + H[j], (XN, ("PMu", H[j][0] // 16, H[j][1] // 16)))
-            m1(*H[j])
-            mm(hb[j], "I", ("M2",) + H[j], False, True)
-            if j < 2:
-                mm(j, "I", ("M1",) + H[j], False, False)
-        for j in range(3):
-            act(("Dm",) + H[j], bank(hb[j], H[j][1] - H[j][0]), ACT.Relu)
-        mm(0, "nI", ("Dm",) + H[0], False, True)
-        m1(*O[0])
-        mm(3, "I", ("M1",) + O[0], True, False)
-        mm(1, "nI", ("Dm",) + H[1], False, True)
-        m2(*O[0])
-        mm(3, "nI", ("M2",) + O[0], False, True)
-        mm(2, "nI", (x,) + H[2], True, False)
-        mm(2, "I", ("M1",) + H[2], False, False)
-        mm(2, "nI", ("Dm",) + H[2], False, True)
-        for j in range(3):
-            act(("Dv",) + H[j], bank(j, H[j][1] - H[j][0]))
-        act(("Dv",) + O[0], bank(3, O[0][1] - O[0][0]))
-        for j in (1, 2):
-            m1(*O[j])
-            mm(3 + j, "I", ("M1",) + O[j], True, False)
-            m2(*O[j])
-            mm(3 + j, "nI", ("M2",) + O[j], False, True)
-        act(("Dv",) + O[1], bank(4, O[1][1] - O[1][0]))
-        cp(("Mu", P0, P1), ("Mi", P0, P1))
-        cp(("Dv",) + O[2], bank(5, O[2][1] - O[2][0]))
-        wrap(7, 0, "Zs", "Dv", E, K, True, False)
-        if t == 0:
-            dma("S", T.Mi[:, 2 * K:RO * K], T.mate[:, 2 * K:RO * K], [("Mu", 0, K)], [("Mi", 2 * K, RO * K)], group())
-        wrap(6, 0, "Zs", "Dv", 0, E, True, False)
-        for lo, hi, bk in ((0, E, 6), (E, K, 7)):
-            mid = (lo + hi) // 2
-            cp(("Dm", 16 * lo, 16 * mid), (("Dv", 0, V), ("Mu", P0 + lo, P0 + mid)))
-            act(("Dm", 16 * mid, 16 * hi), (("Dv", 0, V), ("Mu", P0 + mid, P0 + hi)))
-            wrap(bk, 0, "Zs", "Dm", lo, hi, False, True)
-        for lo, hi, bk in ((0, E, 6), (E, K, 7)):
-            ts(("b1", lo, hi), bank(bk, hi - lo), 0.0, None, ALU.is_gt)
-            tt(("b1", K + lo, K + hi), ("b1", lo, hi), ("dS", lo, hi), ALU.mult)
-            if lo:
-                tt(("b1", 2 * K, 3 * K), ("b1", 0, K), ("dP", 0, K), ALU.mult)
-            tt(("Si", lo, hi), ("b1", K + lo, K + hi), ("vv", lo, hi), ALU.add)
-        cp(("Su", P0, P1), ("Si", 0, K))
-        send(nxt, e_nxt, ("Sg", P0, P1), ("Su", P0, P1), "sg%d" % t)
-        arrive(("Sg", P0, P1), "sg%d" % t, n_small)
-        tt(("Pf", P1, P1 + K), ("b1", 2 * K, 3 * K), ("Pf", P0, P1), ALU.add)
-        cp(("Pu", P1, P1 + K), ("Pf", P1, P1 + K))
-        b0 = t * 2 * K
-        if t == 0:
-            wrap(0, 0, "Za", "Y", 0, K, True, True)
-            wrap(0, K, "Zb", "Y", 0, K, True, True)
-        else:
-            act(("G", 0, V), (("W", 0, V), ("Bk", b0 - K, b0)))
-            wrap(6, 0, "Za", "G", 0, K, True, True)
+        for lo, hi, j in [p for p in ((0, EP, 0), (EP, K, 1)) if p[0] < p[1]]:
+            gathers("pm", "Gp", "Wp", F, lo, hi)
+            wrap(7 - j, 0, "Zp", "Gp", lo, hi, True, True)
+            cp(("PMu", lo, hi), bank(7 - j, hi - lo), name=(t, "pmu%d" % j))
+            tt(("dP", lo, hi), bank(7 - j, hi - lo), sl("Pf", t, lo, hi), ALU.subtract, name=(t, "dp%d" % j))
+        if t:
+            gathers("g", "G", "W", Bf)
+            wrap(7, 0, "Za", "G", 0, K, True, True)
+            cp(sl("Bn", t), bank(7, K), name=(t, "bn"))
             if more:
-                wrap(7, 0, "Zb", "G", 0, K, True, True)
+                columns(7, 6, 0, t)
+                ts(sl("Bf", t + 1), bank(6, K), 7.5 * K, None, ALU.add, name=(t, "bf"))
+        for k, (a, b) in enumerate(PIECES["s"]):
+            tt(w("M1", a, b), (X, sl(P[0], P[1], a, b)), w(xp, a, b), ALU.max, name=(t, "s%d" % k))
+        for k, (a, b) in enumerate(PIECES["t"]):
+            bk = bank(k, 16 * (b - a))
+            if "t%d" % k not in mine:
+                act(w("M2", a, b), (X, ("PMu", a, b)), name=(t, "t%d" % k))
+                mm(k, "nI", w(xp, a, b), True, False)
+                mm(k, "I", w("M2", a, b), False, True)
+                act(w("C", a, b), bk, ACT.Relu, name=(t, "r%d" % k))
+                mm(k, "I", w(xp, a, b), True, False)
+                mm(k, "nI", w("M1", a, b), False, False)
+                mm(k, "I", w("C", a, b), False, True)
+            else:
+                mm(k, "nI", w("M1", a, b), True, False)
+                tt(w("M2", a, b), (X, ("PMu", a, b)), w(xp, a, b), ALU.max, name=(t, "t%d" % k))
+                mm(k, "I", w("M2", a, b), False, True)
+            on("dv%d" % k)(w("Dv", a, b), bk, name=(t, "dv%d" % k))
+        for lo, hi, j in parts:
+            n = hi - lo
+            go = bank(j, n, K)
+            wrap(j, 0, "Zs", "Dv", lo, hi, True, False)
+            gathers("dm", "Dm", "Dv", M, lo, hi)
+            wrap(j, 0, "Zs", "Dm", lo, hi, False, True)
+            ts(go, bank(j, n), 0.0, None, ALU.is_lt, name=(t, "go%d" % j))
+            for d in range(2):
+                tt(sl("Sd", d, lo, hi), go, sl("Ld", 2 + 2 * t + d, lo, hi), ALU.mult, name=(t, "s%s%d" % ("ab"[d], j)))
+            for buf in ("vd", "Sd"):
+                mm(2 + j, "sI", sl(buf, 0, lo, hi), buf == "vd", False)
+                mm(2 + j, "I", sl(buf, 1, lo, hi), False, buf == "Sd")
+            cp(("Su", lo, hi), bank(2 + j, n), name=(t, "su%d" % j))
+            gathers("z", "Z", xp, ("Su", 0), lo, hi)
+            tt(bank(j, n), go, ("dP", lo, hi), ALU.mult, name=(t, "ch%d" % j))
+            tt(sl("Pf", t + 1, lo, hi), bank(j, n), sl("Pf", t, lo, hi), ALU.add, name=(t, "pf%d" % j))
+            cp(sl("Pu", t, lo, hi), sl("Pf", t + 1, lo, hi), name=(t, "pu%d" % j))
+            gathers("u", "U", x, ("Pu", t), lo, hi)
         if more:
-            link_digits(t + 1, group())
+            gd, gs = group(), group()
+            on("hi")(sl("Pd", 2 * t), sl("Pf", t + 1), name=(t, "hi"))
+            tt(sl("Pd", 2 * t + 1), sl("Pf", t + 1), sl("Pd", 2 * t), ALU.subtract, name=(t, "lo"))
+            for d in range(2):
+                flatten("Wp", 4 + d, sl("Pd", 2 * t + d), gd)
+            for d in range(2):
+                flatten("W", d, sl("Sd", d), gs)
         else:
             out = group()
-            dma("S", T.yp[:], T.Pf[:, P1:P1 + K], [("Pf", P1, P1 + K)], [], out)
-        u0 = 0 if t else 48
-        if t == 0:
-            tt(("U", 0, 16 * u0), (XN, ("Pu", P1, P1 + u0)), ("X2", 0, 16 * u0), ALU.add)
-            cp(("B0", 0, 2 * K), bank(0, 2 * K))
-            send(nxt, e_nxt, ("Bk", 0, 2 * K), ("B0", 0, 2 * K), "bk")
-            arrive(("Bk", 0, 2 * K), "bk", n_small)
-        tt(("U", 16 * u0, V), (XN, ("Pu", P1 + u0, P1 + K)), ("X2", 16 * u0, V), ALU.add)
-        if t:
-            cp(("Bk", b0, b0 + K), bank(6, K))
-        act(("Y", 0, 16 * YS[t]), (XP, ("Sg", P0, P0 + YS[t])))
-        if YS[t] < K:
-            cp(("Y", 16 * YS[t], V), (XP, ("Sg", P0 + YS[t], P1)))
-        for k, (a, b) in enumerate(SEG[:-1]):
-            mm(k, "I", (x, a, b), True, False)
-
-        def step(k):
-            a, b = SEG[k]
-            tt(("M1", a, b), (("Y", 0, V), ("Bk", b0 + a // 16, b0 + b // 16)), ("U", a, b), ALU.add)
-
-        step(0)
-        for k, (a, b) in enumerate(SEG):
-            if k + 1 < len(SEG):
-                step(k + 1)
-            ts(("M1", a, b), ("M1", a, b), -CL, CL, ALU.max, ALU.min)
-            if k == 1 and t and more:
-                cp(("Bk", b0 + K, b0 + 2 * K), bank(7, K))
-            if more and PMC[k]:
-                pm_gather(t + 1, sum(PMC[:k]), sum(PMC[:k + 1]))
-            if k + 1 < len(SEG):
-                mm(k, "I", ("M1", a, b), False, True)
-                act((xo, a, b), bank(k, b - a))
+            stage("S", "tp", T.Pf[:, RO * K:RO * K + K], [sl("Pf", RO)], rank, up, 512 * K)
+            trade(["tp"], rank, up, 128 * K)
+        gathers("y", "Y", "Z", Bn)
+        for k, (a, b) in enumerate(PIECES["y"]):
+            bk = bank(k, 16 * (b - a))
+            mm(k, "n2", w(x, a, b), True, False)
+            mm(k, ("I", B), w("U", a, b), False, False)
+            mm(k, "I", w("Y", a, b), False, True)
+            if "e%d" % k in mine:
+                ts(bk, bk, -CL, CL, ALU.max, ALU.min, name=(t, "c%d" % k))
+                tt(w(xo, a, b), bk, w(x, a, b), ALU.add, name=(t, "e%d" % k))
             else:
-                tt((xo, a, b), ("M1", a, b), (x, a, b), ALU.add)
+                ts(w("C", a, b), bk, -CL, CL, ALU.max, ALU.min, name=(t, "c%d" % k))
+                mm(k, "I", w(x, a, b), True, False)
+                mm(k, "I", w("C", a, b), False, True)
+                act(w(xo, a, b), bk, name=(t, "e%d" % k))
+        for j, (c, d) in enumerate(XP if more else OUT):
             if more:
-                send_piece(t + 1, k, a, b)
+                grp = group()
+                for o, i in ((slice(B, 128), slice(0, 128 - B)), (slice(0, B), slice(128 - B, 128))):
+                    dma("S", T["p%d" % (t + 1)][o, 16 * c:16 * d], T[xo][i, 16 * c:16 * d], [w(xo, c, d)],
+                        [w("p%d" % (t + 1), c, d)], 4096 * (d - c), grp)
             else:
-                dma("S", T.yx[:, a:b], T[xo][:, a:b], [(xo, a, b)], [], out)
-        if more:
-            pm_gather(t + 1, C1, K)
-            pm_wrap()
-            ts(("Di", 0, K), ("Si", 0, K), 4, None, ALU.arith_shift_right)
-            ts(("Di", K, 2 * K), ("Si", 0, K), 15, None, ALU.bitwise_and)
-            cp(("Dg", b0, b0 + 2 * K), ("Di", 0, 2 * K))
-            send_forward(t + 1, len(SEG), (b0, b0 + 2 * K))
-            flatten(0, ("Dr", b0, b0 + K), ("Dr", b0 + K, b0 + 2 * K), group())
-            if t + 2 < RO:
-                places(t + 2)
-            ts(("X2", 0, V), (xo, 0, V), -2.0, None, ALU.mult)
-            pm_lists(t + 1)
-    emit(ops, g, T)
+                stage("S", "to%d" % j, T[xo][:, 16 * c:16 * d], [w(xo, c, d)], rank, rank, 4096 * (d - c))
+                trade(["to%d" % j], rank, rank, 1024 * (d - c))
+        if not more:
+            dma("S", T.yp[:], places("tp"), landed("tp"), [], 512 * K, out)
+            for j, (c, d) in enumerate(OUT):
+                dma("S", T.yx[:, 16 * c:16 * d], places("to%d" % j), landed("to%d" % j), [], 4096 * (d - c), out)
+    for j, q in enumerate("VA"):
+        for t in range(RO):
+            for name in LINES[t][j].split():
+                lines[q].append(named.pop((t + 1, name[:-1]) if name[-1] == "+" else (t, name)))
+    assert not named
+    emit(order(ops, lines.values()), g, T)

from concourse.mybir import AluOpType as ALU, ActivationFunctionType as ACT
from concourse.bass import DstId, RemoteDMATransfer

V = 2560
K = V // 16
RO = 4
CL = 10.0
NR = 4
B = 128 // NR
XIN = [(0, 1536), (1536, V)]
ROUND = 1.5 * 2 ** 23
E = 64
EP = 64
SC = 112
PIECES = {
    "pm": [(0, 32), (32, 64), (64, 112), (112, 160)],
    "s": [(0, 64), (64, 96), (96, 160)],
    "t": [(0, 32), (32, 64), (64, 96), (96, 128), (128, 144), (144, 160)],
    "dm": [(0, 32), (32, 64), (64, 112), (112, 160)],
    "u": [(0, 32), (32, 64), (64, 112), (112, 136), (136, 160)],
    "z": [(0, 32), (32, 64), (64, 112), (112, 160)],
    "g": [(0, 32), (32, 64), (64, 96), (96, 128), (128, 160)],
    "y": [(0, 32), (32, 64), (64, 96), (96, 128), (128, 144), (144, 160)],
}
XP = [(0, 64), (64, 96), (96, 160)]
OUT = [(0, 64), (64, 128), (128, 160)]
FIRST = ("s0 pmu0 s1 s2 pmu1 dp0 t2 t3 t4 t5 dv3 dv4 dm0 dm2 go0 dp1 sa0 sb0 ch0 pf0 go1 su0 sa1 sb1 ch1 pu0 pf1 u1 su1 pu1 lo z2 u2 y0 y2 c1 c0 c2 e0 c3 y5 c4 g3+ c5 e4 e5",
         "pm0 pm1 pm2 pm3 t0 t1 r0 r1 dv0 dv2 dv1 dv5 dm1 dm3 z0 hi z1 z3 u0 y1 y3 y4 u3 pm0+ e1 pm1+ e2 e3")
MID = ("pmu0 s0 s1 pmu1 dp0 t2 s2 t3 t4 t5 dv3 dv4 dm0 dm2 go0 dp1 sa0 sb0 ch0 pf0 go1 su0 sa1 sb1 ch1 pu0 pf1 u1 su1 pu1 bn lo z2 u2 y0 y2 c1 c0 c2 e0 c3 bf y5 c4 g3+ c5 e4 e5",
       "pm2 pm3 t0 g1 t1 r0 r1 g0 dv0 dv2 dv1 dv5 dm1 dm3 g2 z0 hi z1 z3 u0 y1 y3 y4 u3 pm0+ e1 pm1+ e2 e3")
LAST = ("pmu0 s0 s1 pmu1 dp0 t2 s2 t3 t4 t5 dv3 dv4 dm0 dm2 go0 dp1 sa0 sb0 ch0 pf0 go1 su0 sa1 sb1 ch1 pu0 pf1 u1 su1 pu1 bn z2 u2 y0 y2 c1 c0 c2 e0 c3 y5 c4 c5 e4 e5",
        "pm2 pm3 t0 g1 t1 r0 r1 g0 dv0 dv2 dv1 dv5 dm1 dm3 g2 z0 z1 z3 u0 y1 y3 y4 u3 e1 e2 e3")
FIRST = ('pm0 bn s0 pmu0 s2 pmu1 s1 t2 t3 bf t5 t4 dv5 dv4 dp0 df0 dp1 go0 sa0 sb0 ch0 su0 pf0 go1 sa1 sb1 ch1 pu0 pf1 su1 u1 pu1 z2 lo y0 u3 c1 c0 e1 e0 c3 c5 c2 e5 c4 e2 e4 e3',
         'pm1 pm3 pm2 t0 fa t1 fb r0 fc r1 dv0 dv2 dv3 dv1 dm2 dm1 z0 z1 z3 hi u0 y1 u2 y3 u4 y5 y2 y4 pm1+')
MID = ('s0 pmu0 dp0 t1 t0 s1 pmu1 s2 t2 t3 t4 t5 dv4 dp1 df0 go0 sa0 sb0 ch0 pf0 su0 pu0 go1 u1 sa1 sb1 ch1 bn pf1 su1 hi z2 pu1 lo y0 u3 c1 c0 e1 e0 u4 c2 c3 e2 e3 c5 c4 e5 e4 bf',
       'pm0 pm3 pm2 g0 g1 g2 g3 g4 dv0 dv1 dv2 dv3 dv5 dm2 dm1 z1 z0 u0 z3 y1 y2 fa u2 y3 fb y5 y4 fc pm1+')
LAST = ('s0 pmu0 t1 t0 pmu1 s1 t2 s2 t3 t5 t4 dv5 dv4 df0 dp0 go0 sa0 sb0 ch0 pf0 su0 pu0 dp1 go1 sa1 sb1 ch1 u1 su1 z2 pf1 bn pu1 y0 u3 c1 c0 e0 c2 e2 c3 e3 c4 c5 e4 e5',
        'pm0 pm3 pm2 g2 g4 g0 g3 dv0 dv1 g1 dv2 dv3 dm1 dm2 z0 u0 z1 z3 y1 u2 y2 y3 e1 u4 y4 y5')
FIRST = ('pm0 bn s0 pmu0 s1 s2 pmu1 dp1 t2 t3 bf t4 t5 dp0 dv4 dv5 dm0 dm2 go0 sa0 sb0 ch0 su0 go1 pf0 sa1 sb1 ch1 pu0 pf1 su1 u1 z2 lo y5 pu1 y0 u3 c1 c0 e1 e0 c5 c3 c2 e5 e2 c4 e3 e4',
         'pm1 pm3 pm2 t0 t1 fa r0 fb r1 fc dv0 dv2 dv1 dv3 dm1 dm3 z0 z1 u0 hi z3 y1 u4 u2 y3 y2 pm1+ y4')
MID = ('pmu0 s0 t0 t1 s1 dp0 pmu1 s2 t2 t3 t5 t4 dp1 dv4 dm0 dm2 go0 sa0 sb0 ch0 pf0 su0 pu0 u1 go1 sa1 sb1 ch1 bn pf1 su1 pu1 z2 u3 lo y0 u4 c1 c0 e1 e0 c3 c2 c5 e3 c4 e2 e4 e5 bf',
       'pm0 pm3 pm2 g0 g1 g3 g2 g4 dv1 dv0 dv2 dv3 dv5 dm1 dm3 z1 z0 u0 z3 hi y1 u2 y3 y2 y5 fa y4 fb pm1+ fc')
LAST = ('s0 pmu0 t1 t0 pmu1 s1 t2 s2 t3 t5 t4 dp0 dv5 dv4 dp1 dm0 dm2 go0 sa0 sb0 ch0 su0 pf0 go1 pu0 sa1 sb1 u1 su1 ch1 bn pf1 z2 pu1 y0 u3 c1 c0 e0 c2 e2 c3 e3 c4 c5 e4 e5',
        'pm0 pm2 pm3 g3 g2 g1 dv0 dv1 g0 dv2 g4 dv3 dm1 dm3 z0 z1 u0 z3 y1 u2 y2 y3 e1 u4 y4 y5')
LINES = [FIRST, MID, MID, LAST]
LU = {"P": 0, "F0": 1, "M0": 2, "F1": 3, "M1": 4, "F2": 5, "M2": 6, "F3": 7, "M3": 8, "Bn": 9, "Bf": 10}
CYC, PEC, FIX, SEM = 0.9e-3, 0.6e-3, 0.06, 0.1
GATHER, SCATTER = 1.5, 3.5
DMA_ISSUE, DMA_FIX, DMA_RATE, REM_FIX, REM_RATE, REM_FIRST = 0.1, 1.8, 300e3, 2.0, 50e3, 3.0
SLACK = 0.3

SCRATCH = {}
for _n in ["x0", "x1", "x2", "x3", "x4", "p0", "p1", "p2", "p3", "M1", "M2", "Dv", "Dm", "Y", "U", "W", "Wp", "G", "Gp",
           "Sc", "C", "Z"]:
    SCRATCH[_n] = ("sbuf", [128, V], "bfloat16")
SLOTS = NR * NR + NR - 1
_tr = [("tp", K, "float32"), ("tl", 2 * K, "int32"), ("tu", 6 * K, "uint16"), ("td", 6 * K, "bfloat16"),
       ("tb", 2 * K, "uint16")]
_tr += [("tx%d" % _k, _b - _a, "bfloat16") for _k, (_a, _b) in enumerate(XIN)]
_tr += [("to%d" % _k, 16 * (_b - _a), "bfloat16") for _k, (_a, _b) in enumerate(OUT)]
for _n, _c, _d in _tr:
    SCRATCH[_n] = ("dram", [SLOTS, 128, _c // NR], _d)
for _d, _l in (
        ("int32", {"Po": K, "Pi": K, "Mo": RO * K, "ip": 8, "iq": 8}),
        ("uint16", {"Ou": 11 * K, "Lu": 11 * K, "Su": K, "Pu": RO * K, "PMu": K, "Bn": RO * K, "Bf": RO * K}),
        ("float32", {"Pf": (RO + 1) * K, "dP": K, "Mq": RO * K, "Mr": RO * K, "J": 144, "A1": 144, "A2": 128, "ic": K,
                     "sF": 128, "vF": 128, "Bq": 2 * K, "j8": 8, "a8": 8, "e8": 8, "pm": 8, "wt": 8}),
        ("bfloat16", {"Od": 12 * K, "Ld": 12 * K, "Pd": 2 * RO * K, "go": K, "Sd": 2 * K, "cw": K, "iw": K, "vd": 2 * K, "Mh": RO * K,
                      "Zs": 144, "Za": 144, "nV": 128, "Bh": K, "Zp": 144, "I": 256, "nI": 128, "n2": 128, "kI": 128, "sI": 128,
                      "nS": 128})):
    for _n, _c in _l.items():
        SCRATCH[_n] = ("sbuf", [128, _c], _d)
for _n in range(8):
    SCRATCH["b%d" % _n] = ("psum", [128, 512], "float32")

NDMA = 70
SEMAPHORES = (["cV", "cA", "cP", "cG", "snt"] + ["d%d" % _n for _n in range(NDMA)] + ["r" + _n[0] for _n in _tr])


def bits(lst):
    m = 0
    for e in lst:
        m |= 1 << e
    return m


def emit(ops, g, T):
    Q = {"V": g.vector, "A": g.scalar, "P": g.tensor, "G": g, "S": g.sync}
    hist = {}
    know = {q: 0 for q in Q}
    last = {q: 0 for q in Q}
    done = []
    for n, o in enumerate(ops):
        q = o["q"]
        deps = set()
        if q is not None:
            for (b, c0, c1), wr in [(r, False) for r in o["rd"]] + [(r, True) for r in o["wr"]]:
                for (m, a0, a1, w2) in hist.get(b, []):
                    p = ops[m]
                    shared_bank = SCRATCH[b][0] == "psum" and p["q"] != q
                    if shared_bank or (a0 < c1 and c0 < a1 and (wr or w2)):
                        if q == "P" and p["q"] == "P":
                            continue
                        if o["grp"] is not None and p["grp"] is o["grp"]:
                            continue
                        deps.add(m)
        o["waits"] = []
        for m in sorted(deps, reverse=True):
            if know[q] >> m & 1:
                continue
            o["waits"].append(m)
            ops[m]["used"] = True
            if ops[m]["grp"] is not None:
                ops[m]["grp"]["used"] = True
                for k in ops[m]["grp"]["ops"]:
                    know[q] |= done[k]
            else:
                know[q] |= done[m]
        d = (know[q] if q is not None else 0) | (1 << n)
        if o["kind"] == "c":
            d |= last[q]
            last[q] = d
        done.append(d)
        if o["kind"] != "r":
            for r, wr in [(r, False) for r in o["rd"]] + [(r, True) for r in o["wr"]]:
                h = hist.setdefault(r[0], [])
                if wr:
                    h[:] = [e for e in h if not (r[1] <= e[1] and e[2] <= r[2] and (
                        (q is not None and know[q] >> e[0] & 1) or (q == "P" and ops[e[0]]["q"] == "P")))]
                h.append((n, r[1], r[2], wr))
    cnt = {}
    for o in ops:
        if o["kind"] == "c" and o["used"]:
            s = "c" + o["q"]
            cnt[s] = cnt.get(s, 0) + 1
            o["tok"] = (s, cnt[s])
        elif o["kind"] == "d":
            o["tok"] = (o["grp"]["sem"], 16 * len(o["grp"]["ops"]))
    sent = 0
    for o in ops:
        if o["q"] is None:
            continue
        e = Q[o["q"]]
        for m in o["waits"]:
            e.wait_ge(T.sem[ops[m]["tok"][0]], ops[m]["tok"][1])
        ins = o["fn"](e)
        if o["kind"] == "c" and o["used"]:
            ins.then_inc(T.sem[o["tok"][0]], 1)
        elif o["kind"] == "d":
            ins.then_inc(T.sem[o["tok"][0]], 16)
        elif o["kind"] == "r":
            sent += o["n"]
    g.wait_ge(T.sem.snt, sent)
    seen = set()
    for o in ops:
        left = (o["kind"] == "d" and not o["grp"]["used"]) or (o["kind"] == "e" and not o["used"])
        if left and o["tok"] not in seen:
            seen.add(o["tok"])
            g.wait_ge(T.sem[o["tok"][0]], o["tok"][1])


def order(ops, lines):
    n = len(ops)
    deps = [dict() for _ in ops]
    hist = {}
    for i, o in enumerate(ops):
        if o["kind"] == "e":
            deps[i][o["after"]] = True
        for r, wr in [(r, False) for r in o["rd"]] + [(r, True) for r in o["wr"]]:
            h = hist.setdefault(r[0], [])
            psum = SCRATCH[r[0]][0] == "psum"
            for (m, a0, a1, w2) in h:
                p = ops[m]
                if m == i or o["kind"] == "e" or (o["grp"] is not None and p["grp"] is o["grp"]):
                    continue
                meet = a0 < r[2] and r[1] < a1 and (wr or w2)
                if meet or psum:
                    hard = not (p["q"] == o["q"] and (o["q"] == "P" or not meet))
                    for k in (p["grp"]["ops"] if p["grp"] else [m]):
                        deps[i][k] = deps[i].get(k, False) or hard
            if o["kind"] != "r":
                if wr and o["grp"] is None:
                    h[:] = [e for e in h if not (r[1] <= e[1] and e[2] <= r[2])]
                h.append((i, r[1], r[2], wr))
    for line in lines:
        for m, i in zip(line, line[1:]):
            deps[i].setdefault(m, False)
    after = [[] for _ in ops]
    for i in range(n):
        for m in deps[i]:
            after[m].append(i)
    left = [len(d) for d in deps]
    topo = [i for i in range(n) if not left[i]]
    for i in topo:
        for j in after[i]:
            left[j] -= 1
            if not left[j]:
                topo.append(j)
    assert len(topo) == n
    chain = [0.0] * n
    for i in reversed(topo):
        o = ops[i]
        chain[i] = o["dur"] + max([chain[j] + (o["lat"] if deps[j][i] else 0.0) for j in after[i]] + [o["lat"]])
    left = [len(d) for d in deps]
    ready = [0.0] * n
    free = {q: 0.0 for q in ["V", "A", "P", "G", "S", None]}
    cand = {q: [] for q in free}
    for i in range(n):
        if not left[i]:
            cand[ops[i]["q"]].append(i)
    out = []
    while len(out) < n:
        t0, q = min((max(free[q], min(ready[i] for i in c)), q or "") for q, c in cand.items() if c)
        q = q or None
        i = max((i for i in cand[q] if ready[i] <= t0 + SLACK), key=lambda i: (chain[i], -i))
        o = ops[i]
        cand[q].remove(i)
        end = max(free[q], ready[i]) + o["dur"]
        if q:
            free[q] = end
        out.append(i)
        for j in after[i]:
            ready[j] = max(ready[j], end + (o["lat"] if deps[j][i] else 0.0))
            left[j] -= 1
            if not left[j]:
                cand[ops[j]["q"]].append(j)
    place = {m: k for k, m in enumerate(out)}
    for grp in [o["grp"] for k, o in enumerate(ops) if o["grp"] is not None and o["grp"]["ops"][0] == k]:
        grp["ops"][:] = [place[m] for m in grp["ops"]]
    return [ops[m] for m in out]


def engine_shares(rank, T, topo):
    core = T.cores[rank]
    others = [r for r in range(len(T.cores)) if r != rank]
    far = [r for r in others if T.cores[r] not in topo.cores_of(core)]
    share, taken = {}, []
    for j, r in enumerate(far):
        e = topo.engines(core, T.cores[r])
        n = len(e) // len(far)
        share[r] = e[j * n:(j + 1) * n]
        taken += share[r]
    for r in others:
        if r not in far:
            share[r] = [e for e in topo.engines(core, T.cores[r]) if e not in taken]
    return share


def rank_program(g, core, T, topo):
    rank = T.rank_of(core)
    if rank is None:
        return
    share = engine_shares(rank, T, topo)
    others = sorted(share)
    come = sum(len(engine_shares(r, T, topo)[rank]) for r in others)
    up = (rank + 1) % NR

    ops = []
    ngrp = [0]
    sends = []
    lines = {q: [] for q in "VAGS"}
    keep = ["VAGS"]
    named = {}

    def ap(r):
        return T[r[0]][:, r[1]:r[2]]

    def w(name, a, b):
        return (name, 16 * a, 16 * b)

    def sl(name, slot, a=0, b=K):
        return (name, slot * K + a, slot * K + b)

    def rec(q, kind, fn, rd, wr, dur, lat=SEM, grp=None, n=0, tok=None, after=None, name=None):
        o = {"q": q, "kind": kind, "fn": fn, "rd": rd, "wr": wr, "grp": grp, "used": False, "n": n, "tok": tok,
             "dur": dur, "lat": lat, "after": after, "name": name}
        if grp is not None:
            grp["ops"].append(len(ops))
        if name is not None:
            named[name] = len(ops)
        elif q is not None and q in keep[0]:
            lines[q].append(len(ops))
        ops.append(o)

    def group():
        ngrp[0] += 1
        return {"sem": "d%d" % (ngrp[0] - 1), "ops": [], "used": False}

    def bank(b, n=512, o=0):
        return ("b%d" % b, o, o + n)

    def src(r):
        if len(r) == 2:
            return ap(r[0]).indirect(ap(r[1])), [r[0], r[1]]
        return ap(r), [r]

    def cost(o, a, cycles=1.0):
        return FIX + CYC * max(64, (o[2] - o[1]) * (GATHER if len(a) == 2 else cycles))

    def tt(o, a, b, op, name=None):
        pa, ra = src(a)
        both = all(SCRATCH[r[0]][0] == "sbuf" for r in ra + [b])
        rec("V", "c", lambda e: e.tensor_tensor(ap(o), pa, ap(b), op), ra + [b], [o], cost(o, a, 2.0 if both else 1.0),
            name=name)

    def ts(o, a, s1, s2, op0, op1=None, name=None):
        more = [] if op1 is None else [op1]
        rec("V", "c", lambda e: e.tensor_scalar(ap(o), ap(a), s1, s2, op0, *more), [a], [o], cost(o, a), name=name)

    def cp(o, a, name=None):
        pa, ra = src(a)
        rec("V", "c", lambda e: e.tensor_copy(ap(o), pa), ra, [o], cost(o, a), name=name)

    def fill(buf):
        rec("V", "c", lambda e: e.memset(T[buf][:], 0.0), [], [(buf, 0, V)], cost((buf, 0, V), (buf, 0, V), 0.5))

    def act(o, a, func=ACT.Copy, scale=None, bias=None, name=None):
        pa, ra = src(a)
        kw = {}
        for key, val in (("scale", scale), ("bias", bias)):
            if isinstance(val, tuple):
                kw[key] = ap(val)
                ra = ra + [val]
            elif val is not None:
                kw[key] = val
        rec("A", "c", lambda e: e.activation(ap(o), pa, func, **kw), ra, [o], cost(o, a), name=name)

    def mm(b, wt, r, start, stop, o=0):
        name, s = wt if isinstance(wt, tuple) else (wt, 0)
        rec("P", "c", lambda e: e.matmul(T["b%d" % b][:, o:o + r[2] - r[1]], T[name][:, s:s + 128], ap(r), start, stop),
            [(name, s, s + 128), r], [bank(b)], PEC * max(64, r[2] - r[1]), 2 * SEM)

    def wrap(b, oc, z, s, c0, c1, start, stop):
        def four(e, i0):
            for i in range(i0, i0 + 4):
                ins = e.matmul(T["b%d" % b][:, oc:oc + c1 - c0], T[z][:, 15 - i:143 - i],
                               T[s][:, 16 * c0 + i:16 * c1:16], start and i == 0, stop and i == 15)
            return ins
        for i0 in range(0, 16, 4):
            rec("P", "c", lambda e, i0=i0: four(e, i0), [(z, 0, 144), (s, 16 * c0, 16 * c1)], [bank(b)],
                4 * PEC * max(64, c1 - c0), 2 * SEM)

    def dma(q, o, i, rd, wr, size, grp=None):
        rec(q, "d", lambda e: e.dma_start(o, i), rd, wr, DMA_ISSUE, DMA_FIX + size / DMA_RATE, grp or group())

    def flatten(win, row, lst, grp, q="S"):
        dma(q, T[win][row:128:16, :], ap(lst), [lst], [(win, 0, V)], 256 * K, grp)

    def slot(u):
        return NR - 1 + NR * u

    def stage(q, buf, i, rd, mine, kept, size, rows=slice(0, 128), grp=None):
        a = slot(mine) - kept
        dma(q, T[buf][a:a + NR, rows, :], i, rd, [(buf, a, a + NR)], size, grp)

    def places(buf, a=0, b=NR, rows=slice(0, 128)):
        return T[buf][slot(a):slot(b - 1) + 1:NR, rows, :]

    def landed(buf, a=0, b=NR):
        return [(buf, slot(u), slot(u) + 1) for u in range(a, b)]

    def trade(bufs, mine, kept, size):
        trs, rd = [], []
        for r in others:
            rid, pid = topo.addr(T.cores[r], core)
            n = len(share[r]) // len(bufs)
            for j, buf in enumerate(bufs):
                part = slot(mine) - kept + (kept + r - rank) % NR
                rd.append((buf, part, part + 1))
                trs.append(RemoteDMATransfer(dst_ids=[DstId(rid=rid, pnc=pid)],
                                             dma_engine_mask=bits(share[r][j * n:(j + 1) * n]),
                                             remote_sem=T.sem["r" + bufs[0]], src=T[buf][part], dst=T[buf][slot(mine)]))
        sends.append(len(ops))
        rec("G", "r", lambda e: e.remote_dma_fused(trs, local_sem=T.sem.snt), rd, [],
            0.3 + size / REM_RATE + (REM_FIRST if len(sends) == 1 else 0.0), REM_FIX,
            n=sum(len(share[r]) for r in others))
        rec(None, "e", None, [], [r for buf in bufs for u in range(NR) if u != mine for r in landed(buf, u, u + 1)],
            0.0, 0.0, tok=("r" + bufs[0], come), after=sends[-1])

    def iota(o, pattern, base, mult):
        kw = {} if SCRATCH[o[0]][2] == "int32" else {"allow_small_or_imprecise_dtypes": True}
        rec("G", "c", lambda e: e.iota(ap(o), pattern, base, mult, **kw), [], [o], 0.13 + 2 * CYC * (o[2] - o[1]))

    def mate_digits(c, a, b):
        n = K * (b - a)
        ts(sl("Mq", a, 0, n), sl("Mo", a, 0, n), 1.0 / 16, -7.5 / 16, ALU.mult, ALU.add)
        act(sl("Mr", a, 0, n), sl("Mq", a, 0, n), ACT.Identity, bias=("wt", 6, 7))
        act(sl("Mh", a, 0, n), sl("Mr", a, 0, n), ACT.Identity, bias=("wt", 7, 8))
        for t in range(a, b):
            mm(t, "sF", sl("Mq", t), True, False, o=K)
            mm(t, "nS", sl("Mh", t), False, True, o=K)
            mm(t, "I", sl("Mh", t), True, False, o=2 * K)
            mm(t, "nI", sl("vd", 0), False, True, o=2 * K)
        for t in range(a, b):
            act(sl(c + "d", 3 + 2 * t), bank(t, K, K), ACT.Identity, bias=("pm", 2, 3))
            act(sl(c + "d", 2 + 2 * t), bank(t, K, 2 * K))
            mm(t, "I", sl("Mh", t), True, False)
            mm(t, "kI", sl("vd", 1), False, False)
            mm(t, "kI", sl(c + "d", 3 + 2 * t), False, True)

    def mate_lists(c, t):
        cp(sl(c + "u", LU["M%d" % t]), sl("Mo", t))
        cp(sl(c + "u", LU["F%d" % t]), bank(t, K))

    def columns(b, c, o, t):
        act(("Bq", 0, K), bank(b, K), ACT.Identity, scale=1.0 / 16, bias=("pm", 3, 4), name=(t, "fa"))
        act(("Bq", K, 2 * K), ("Bq", 0, K), ACT.Identity, bias=("wt", 6, 7), name=(t, "fb"))
        act(("Bh", 0, K), ("Bq", K, 2 * K), ACT.Identity, bias=("wt", 7, 8), name=(t, "fc"))
        mm(c, "vF", ("Bq", 0, K), True, False, o=o)
        mm(c, "nV", ("Bh", 0, K), False, False, o=o)
        mm(c, "I", ("Bh", 0, K), False, True, o=o)

    def scatter(a, b):
        rec("V", "c", lambda e: e.tensor_copy(T.Y[:, 0:V].indirect(T.Ou[:, a:b]), T.Sc[:, 16 * a:16 * b]),
            [w("Sc", a, b), ("Ou", a, b)], [("Y", 0, V)], FIX + CYC * SCATTER * 16 * (b - a))

    def land_x(h, name):
        (a, b), buf, grp = XIN[h], "tx%d" % h, group()
        if name == "x0":
            dma("S", T.x0[:, a:b], places(buf), landed(buf), [("x0", a, b)], 256 * (b - a), grp)
        else:
            dma("S", T.p0[B:128, a:b], places(buf, 0, NR - 1), landed(buf), [("p0", a, b)], 256 * (b - a), grp)
            dma("S", T.p0[0:B, a:b], places(buf, NR - 1, NR), landed(buf), [("p0", a, b)], 256 * (b - a), grp)

    g1, g3, g4, g5, g6 = group(), group(), group(), group(), group()
    stage("S", "tl", T.p[:], [], up, rank, 512 * K, slice(0, 64), g1)
    stage("A", "tl", T.mate[:, 0:K], [], up, rank, 512 * K, slice(64, 128), g1)
    dma("S", T.Po[:], T.p[:], [], [("Po", 0, K)], 512 * K)
    dma("A", T.Mo[:, K:RO * K], T.mate[:, K:RO * K], [], [("Mo", K, RO * K)], 2048 * K)
    iota(("ip", 0, 8), [[0, 8]], 0, 1)
    iota(("ic", 0, K), [[1, K // 16], [0, 16]], 0, 0)
    iota(("iw", 0, K), [[0, K // 16], [1, 16]], 0, 0)
    iota(("J", 0, 144), [[1, 144]], -15, -1)
    iota(("j8", 0, 8), [[-1, 8]], 0, 0)
    iota(("vd", 0, K), [[1, K]], 0, 0)
    trade(["tl"], up, rank, 256 * K)
    pm = ("pm", 0, 1)
    ts(("iq", 0, 8), ("ip", 0, 8), 15, None, ALU.bitwise_and)
    cp(("pm", 0, 8), ("iq", 0, 8))
    fill("Sc")
    act(("wt", 0, 1), pm, ACT.Identity, scale=float(K // 16))
    act(("cw", 0, K), ("ic", 0, K), ACT.Identity, bias=("wt", 0, 1))
    flatten("Sc", 0, ("cw", 0, K), g3)
    flatten("Sc", 1, ("iw", 0, K), g3)
    for h, (a, b) in enumerate(XIN):
        stage("S", "tx%d" % h, T.x[:, a:b], [], rank, rank, 512 * (b - a))
        trade(["tx%d" % h], rank, rank, 64 * (b - a))
    ts(("wt", 6, 7), pm, 0.0, ROUND, ALU.mult, ALU.add)
    ts(("wt", 7, 8), pm, 0.0, -ROUND, ALU.mult, ALU.add)
    ts(("pm", 2, 3), pm, -1.0, 7.5, ALU.mult, ALU.add)
    ts(("pm", 3, 4), pm, 0.0, -7.5 / 16, ALU.mult, ALU.add)
    fill("Wp")
    cp(sl("Ou", 0), ("Po", 0, K))
    act(("A2", 0, 128), ("J", 15, 143), ACT.Abs)
    act(("a8", 0, 8), ("j8", 0, 8), ACT.Abs, bias=pm)
    act(("A1", 0, 144), ("J", 0, 144), ACT.Abs, bias=pm)
    act(("I", 0, 128), ("A2", 0, 128), ACT.Relu, scale=-1.0, bias=1.0)
    act(("e8", 0, 8), ("a8", 0, 8), ACT.Relu, scale=-1.0, bias=1.0)
    act(("Zs", 0, 144), ("A1", 0, 144), ACT.Relu, scale=-1.0, bias=1.0)
    act(("I", 128, 256), ("A2", 0, 128), ACT.Relu, scale=-1.0, bias=1.0)
    for name, scale in (("kI", K), ("sF", 16), ("nS", -16), ("nI", -1), ("n2", -2), ("sI", 16)):
        act((name, 0, 128), ("I", 0, 128), ACT.Identity, scale=float(scale))
    act(("vd", K, 2 * K), ("ic", 0, K), ACT.Identity, scale=0.0, bias=pm)
    mate_digits("O", 1, RO)
    act(("W", 0, V), ("Wp", 0, V))
    scatter(0, SC)
    act(("wt", 4, 5), ("e8", 0, 1), ACT.Identity, bias=("e8", 2, 3))
    act(("wt", 5, 6), ("e8", 1, 2), ACT.Identity, bias=("e8", 3, 4))
    act(("wt", 3, 4), ("e8", 4, 5), ACT.Identity, bias=("e8", 5, 6))
    act(("wt", 1, 2), ("wt", 4, 5), ACT.Identity, scale=16.0, bias=("wt", 5, 6))
    act(("vF", 0, 128), ("I", 0, 128), ACT.Identity, scale=float(V))
    act(("nV", 0, 128), ("I", 0, 128), ACT.Identity, scale=-float(V))
    act(("Zp", 0, 144), ("Zs", 0, 144), ACT.Identity, scale=("wt", 3, 4))
    act(("Za", 0, 144), ("Zs", 0, 144), ACT.Identity, scale=("wt", 1, 2))
    for t in range(1, RO):
        mate_lists("O", t)
    dma("S", T.Pi[:], places("tl", rows=slice(0, 64)), landed("tl"), [("Pi", 0, K)], 512 * K)
    dma("S", T.Mo[:, 0:K], places("tl", rows=slice(64, 128)), landed("tl"), [sl("Mo", 0)], 512 * K)
    land_x(0, "x0")
    cp(sl("Pf", 0), ("Pi", 0, K))
    cp(sl("Ld", 0), ("Pi", 0, K))
    tt(sl("Ld", 1), sl("Pf", 0), sl("Ld", 0), ALU.subtract)
    for d in range(2):
        flatten("Wp", 4 + d, sl("Ld", d), g5)
    land_x(1, "x0")
    land_x(0, "p0")
    land_x(1, "p0")
    mate_digits("L", 0, 1)
    cp(sl("Lu", LU["P"]), ("Pi", 0, K))
    scatter(SC, K)
    mate_lists("L", 0)
    keep[0] = "GS"
    stage("S", "tu", T.Ou[:, 3 * K:9 * K], [("Ou", 3 * K, 9 * K)], up, rank, 1536 * K, grp=g6)
    stage("S", "td", T.Od[:, 4 * K:10 * K], [("Od", 4 * K, 10 * K)], up, rank, 1536 * K, grp=g6)
    trade(["tu", "td"], up, rank, 768 * K)
    wrap(4, 0, "Za", "Y", 0, K, True, True)
    cp(sl("Ou", LU["Bn"]), bank(4, K), name=(0, "bn"))
    columns(4, 5, 0, 0)
    ts(sl("Ou", LU["Bf"]), bank(5, K), 7.5 * K, None, ALU.add, name=(0, "bf"))
    stage("S", "tb", T.Ou[:, 9 * K:11 * K], [("Ou", 9 * K, 11 * K)], up, rank, 512 * K)
    trade(["tb"], up, rank, 128 * K)
    flatten("W", 2, ("vd", 0, K), g4)
    flatten("W", 3, ("vd", K, 2 * K), g4)
    dma("S", T.Lu[:, 9 * K:11 * K], places("tb"), landed("tb"), [("Lu", 9 * K, 11 * K)], 512 * K)
    dma("S", T.Lu[:, 3 * K:9 * K], places("tu"), landed("tu"), [("Lu", 3 * K, 9 * K)], 1536 * K)
    dma("S", T.Ld[:, 4 * K:10 * K], places("td"), landed("td"), [("Ld", 4 * K, 10 * K)], 1536 * K)

    for t in range(RO):
        x, xo, xp = "x%d" % t, "x%d" % (t + 1), "p%d" % t
        X = (x, 0, V)
        more = t + 1 < RO
        P, Bn = (("Pu", t - 1), ("Bn", t)) if t else (("Lu", LU["P"]), ("Lu", LU["Bn"]))
        Bf = ("Bf", t) if t > 1 else ("Lu", LU["Bf"])
        F, M = ("Lu", LU["F%d" % t]), ("Lu", LU["M%d" % t])
        parts = [p for p in ((0, E, 0), (E, K, 1)) if p[0] < p[1]]
        mine = LINES[t][0].split() + [n[:-1] for n in LINES[t - 1][0].split() if t and n[-1] == "+"]

        def on(name):
            return cp if name in mine else act

        def gathers(kind, out, win, lst, lo=0, hi=K):
            for k, (a, b) in enumerate(PIECES[kind]):
                if lo <= a < hi:
                    name = "%s%d" % (kind, k)
                    on(name)(w(out, a, b), ((win, 0, V), sl(lst[0], lst[1], a, b)), name=(t, name))

        for lo, hi, j in [p for p in ((0, EP, 0), (EP, K, 1)) if p[0] < p[1]]:
            gathers("pm", "Gp", "Wp", F, lo, hi)
            wrap(7 - j, 0, "Zp", "Gp", lo, hi, True, True)
            cp(("PMu", lo, hi), bank(7 - j, hi - lo), name=(t, "pmu%d" % j))
            tt(("dP", lo, hi), bank(7 - j, hi - lo), sl("Pf", t, lo, hi), ALU.subtract, name=(t, "dp%d" % j))
        if t:
            gathers("g", "G", "W", Bf)
            wrap(7, 0, "Za", "G", 0, K, True, True)
            cp(sl("Bn", t), bank(7, K), name=(t, "bn"))
            if more:
                columns(7, 6, 0, t)
                ts(sl("Bf", t + 1), bank(6, K), 7.5 * K, None, ALU.add, name=(t, "bf"))
        for k, (a, b) in enumerate(PIECES["s"]):
            tt(w("M1", a, b), (X, sl(P[0], P[1], a, b)), w(xp, a, b), ALU.max, name=(t, "s%d" % k))
        for k, (a, b) in enumerate(PIECES["t"]):
            bk = bank(k, 16 * (b - a))
            if "t%d" % k not in mine:
                act(w("M2", a, b), (X, ("PMu", a, b)), name=(t, "t%d" % k))
                mm(k, "nI", w(xp, a, b), True, False)
                mm(k, "I", w("M2", a, b), False, True)
                act(w("C", a, b), bk, ACT.Relu, name=(t, "r%d" % k))
                mm(k, "I", w(xp, a, b), True, False)
                mm(k, "nI", w("M1", a, b), False, False)
                mm(k, "I", w("C", a, b), False, True)
            else:
                mm(k, "nI", w("M1", a, b), True, False)
                tt(w("M2", a, b), (X, ("PMu", a, b)), w(xp, a, b), ALU.max, name=(t, "t%d" % k))
                mm(k, "I", w("M2", a, b), False, True)
            on("dv%d" % k)(w("Dv", a, b), bk, name=(t, "dv%d" % k))
        for lo, hi, j in parts:
            n = hi - lo
            go = bank(j, n, K)
            wrap(j, 0, "Zs", "Dv", lo, hi, True, False)
            gathers("dm", "Dm", "Dv", M, lo, hi)
            wrap(j, 0, "Zs", "Dm", lo, hi, False, True)
            ts(go, bank(j, n), 0.0, None, ALU.is_lt, name=(t, "go%d" % j))
            for d in range(2):
                tt(sl("Sd", d, lo, hi), go, sl("Ld", 2 + 2 * t + d, lo, hi), ALU.mult, name=(t, "s%s%d" % ("ab"[d], j)))
            for buf in ("vd", "Sd"):
                mm(2 + j, "sI", sl(buf, 0, lo, hi), buf == "vd", False)
                mm(2 + j, "I", sl(buf, 1, lo, hi), False, buf == "Sd")
            cp(("Su", lo, hi), bank(2 + j, n), name=(t, "su%d" % j))
            gathers("z", "Z", xp, ("Su", 0), lo, hi)
            tt(bank(j, n), go, ("dP", lo, hi), ALU.mult, name=(t, "ch%d" % j))
            tt(sl("Pf", t + 1, lo, hi), bank(j, n), sl("Pf", t, lo, hi), ALU.add, name=(t, "pf%d" % j))
            cp(sl("Pu", t, lo, hi), sl("Pf", t + 1, lo, hi), name=(t, "pu%d" % j))
            gathers("u", "U", x, ("Pu", t), lo, hi)
        if more:
            gd, gs = group(), group()
            on("hi")(sl("Pd", 2 * t), sl("Pf", t + 1), name=(t, "hi"))
            tt(sl("Pd", 2 * t + 1), sl("Pf", t + 1), sl("Pd", 2 * t), ALU.subtract, name=(t, "lo"))
            for d in range(2):
                flatten("Wp", 4 + d, sl("Pd", 2 * t + d), gd)
            for d in range(2):
                flatten("W", d, sl("Sd", d), gs)
        else:
            out = group()
            stage("S", "tp", T.Pf[:, RO * K:RO * K + K], [sl("Pf", RO)], rank, up, 512 * K)
            trade(["tp"], rank, up, 128 * K)
        gathers("y", "Y", "Z", Bn)
        for k, (a, b) in enumerate(PIECES["y"]):
            bk = bank(k, 16 * (b - a))
            mm(k, "n2", w(x, a, b), True, False)
            mm(k, ("I", B), w("U", a, b), False, False)
            mm(k, "I", w("Y", a, b), False, True)
            if "e%d" % k in mine:
                ts(bk, bk, -CL, CL, ALU.max, ALU.min, name=(t, "c%d" % k))
                tt(w(xo, a, b), bk, w(x, a, b), ALU.add, name=(t, "e%d" % k))
            else:
                ts(w("C", a, b), bk, -CL, CL, ALU.max, ALU.min, name=(t, "c%d" % k))
                mm(k, "I", w(x, a, b), True, False)
                mm(k, "I", w("C", a, b), False, True)
                act(w(xo, a, b), bk, name=(t, "e%d" % k))
        for j, (c, d) in enumerate(XP if more else OUT):
            if more:
                grp = group()
                for o, i in ((slice(B, 128), slice(0, 128 - B)), (slice(0, B), slice(128 - B, 128))):
                    dma("S", T["p%d" % (t + 1)][o, 16 * c:16 * d], T[xo][i, 16 * c:16 * d], [w(xo, c, d)],
                        [w("p%d" % (t + 1), c, d)], 4096 * (d - c), grp)
            else:
                stage("S", "to%d" % j, T[xo][:, 16 * c:16 * d], [w(xo, c, d)], rank, rank, 4096 * (d - c))
                trade(["to%d" % j], rank, rank, 1024 * (d - c))
        if not more:
            dma("S", T.yp[:], places("tp"), landed("tp"), [], 512 * K, out)
            for j, (c, d) in enumerate(OUT):
                dma("S", T.yx[:, 16 * c:16 * d], places("to%d" % j), landed("to%d" % j), [], 4096 * (d - c), out)
    for j, q in enumerate("VA"):
        for t in range(RO):
            for name in LINES[t][j].split():
                lines[q].append(named.pop((t + 1, name[:-1]) if name[-1] == "+" else (t, name)))
    assert not named
    emit(order(ops, lines.values()), g, T)
